import numpy as np
import ml_dtypes


def mxq(x, axis, fmt="e4m3"):
    dtype, down = {"e4m3": (ml_dtypes.float8_e4m3fn, 7), "e5m2": (ml_dtypes.float8_e5m2, 14)}[fmt]
    v = np.moveaxis(np.asarray(x, np.float32).astype(ml_dtypes.bfloat16).astype(np.float64), axis, -1)
    blocks = v.reshape(v.shape[:-1] + (-1, 32))
    amax = np.abs(blocks).max(-1, keepdims=True)
    byte = np.maximum(np.where(amax > 0, np.frexp(amax)[1] - 1 + 127, 0) - down, 1)
    scale = np.exp2(byte - 127.0)
    codes = (blocks / scale).astype(np.float32).astype(dtype).astype(np.float64)
    return np.moveaxis((codes * scale).reshape(v.shape), -1, axis)


WIDE = False


def mx_kscale(k):
    if not WIDE:
        return np.ones(k)
    levels = np.array([10, -10, 5, -5, 0])
    if k % 512:
        return np.exp2(np.random.permutation(np.resize(levels, k // 32))).repeat(32)
    a = np.empty((k // 512, 16))
    for p in range(k // 512):
        a[p, :8] = np.random.permutation(np.resize(levels, 8))
        for g in range(8):
            far = levels[np.abs(levels - a[p, g]) >= 10]
            a[p, g + 8] = far[np.random.randint(len(far))]
    return np.exp2(a.ravel()).repeat(32)


def f64(x):
    return np.asarray(x).astype(np.float64)


def striped(idx):
    return np.tile(idx.reshape(-1, 16).T, (8, 1)).astype(np.uint16)


def unstriped(offs):
    return offs[:16].T.reshape(-1).astype(np.int64)


def striped8(idx):
    return np.concatenate([x.reshape(-1, 16).T for x in idx]).astype(np.uint16)


def runs(offs, k):
    lists = np.stack([offs[16 * r : 16 * r + 16].T.reshape(-1) for r in range(8)]).astype(np.int64)
    return lists[np.arange(k) % 512 // 64]


def pack_weight(w):
    k, n = w.shape
    w = f64(np.asarray(w, np.float32).astype(ml_dtypes.bfloat16)).reshape(k // 32, 32, n)
    amax = np.abs(w).max(1)
    byte = np.clip(np.where(amax > 0, np.frexp(amax)[1] - 1 + 127 - 7, 1), 1, 254)
    scaled = (w * np.exp2(127.0 - byte)[:, None, :]).reshape(k, n).astype(np.float32)
    words = np.ascontiguousarray(scaled.reshape(k // 512, 128, 4, n).transpose(0, 1, 3, 2)).astype(ml_dtypes.float8_e4m3fn).view(np.uint8)
    return words, np.ascontiguousarray(byte.astype(np.uint8).reshape(k // 512, 16, n))


def unpack_weight(words, scales):
    g, p, n, _ = words.shape
    vals = np.ascontiguousarray(words).view(ml_dtypes.float8_e4m3fn).astype(np.float64) * np.repeat(np.exp2(scales.astype(np.float64) - 127.0), 8, axis=1)[..., None]
    return vals.transpose(0, 1, 3, 2).reshape(g * 512, n)


K, T, S, N, U = 512, 2048, 512, 512, 1024


def setup_inputs():
    n = np.random.standard_normal
    s = mx_kscale(K)[:, None]
    packed_xT = pack_weight(n((K, T)) * s)
    return {
        "x_words": packed_xT[0],
        "x_scales": packed_xT[1],
        "w1": (n((K, N)) / np.sqrt(K) / s).astype(np.float32),
        "par": n((N, U)).astype(np.float32),
        "vel": n((N, U)).astype(np.float32),
        "offs": striped(np.random.permutation(T)[:S]),
        "ent": striped8(np.stack([np.random.permutation(U)[:S] for _ in range(8)])),
    }


def reference(x_words, x_scales, w1, par, vel, offs, ent):
    xq = unpack_weight(x_words, x_scales)[:, unstriped(offs)]
    y = mxq(f64(w1), 0, "e4m3").T @ xq
    a = 0.75 * (f64(vel)[np.arange(N)[:, None], runs(ent, N)]) - (0.25 * y)
    o = f64(par)[np.arange(N)[:, None], runs(ent, N)] + 0.75 * a - (0.25 * y)
    out = f64(par).copy()
    out[np.arange(N)[:, None], runs(ent, N)] = o
    return out

@@ -1,0 +1,133 @@
+from contextlib import ExitStack
+
+import concourse.mybir as mybir
+from concourse.masks import make_identity
+
+K, T, S, N, U = 512, 2048, 512, 512, 1024
+FLOPS = 2 * K * N * S
+
+F32 = mybir.dt.float32
+BF16 = mybir.dt.bfloat16
+I32 = mybir.dt.int32
+U32 = mybir.dt.uint32
+U16 = mybir.dt.uint16
+U8 = mybir.dt.uint8
+FP8X4 = mybir.dt.float8_e4m3fn_x4
+MULT = mybir.AluOpType.mult
+ADD = mybir.AluOpType.add
+COPY = mybir.ActivationFunctionType.Copy
+
+P = 128
+PACK = 4
+TILES = N // P
+BANK = 512
+VEL_FACTOR = 0.75 * 0.75
+GRAD_FACTOR = -(0.75 * 0.25 + 0.25)
+
+
+def tile_picked_snag_none_p_kernel(tc, x_words, x_scales, w1, par, vel, offs, ent, out):
+    nc = tc.nc
+    with ExitStack() as ctx:
+        keep = ctx.enter_context(tc.tile_pool(name="keep", bufs=1))
+        psum = ctx.enter_context(tc.psum_pool(name="psum", bufs=2))
+        work = ctx.enter_context(tc.tile_pool(name="work", bufs=2))
+
+        offs_sb = keep.tile([P, S // 16], U16, name="offs_sb")
+        ent_sb = keep.tile([P, S // 16], U16, name="ent_sb")
+        w_raw = keep.tile([P, PACK, N], F32, name="w_raw")
+        x_table = keep.tile([P, T], I32, name="x_table")
+        xs_table = keep.tile([P, T], U8, name="xs_table")
+        vel_sb = [keep.tile([P, U], F32, name="vel_sb%d" % t) for t in range(TILES)]
+        par_sb = [keep.tile([P, U], F32, name="par_sb%d" % t) for t in range(TILES)]
+
+        nc.vector.memset(xs_table[:].bitcast(I32), 0)
+        for q in range(4):
+            nc.sync.dma_start(
+                out=xs_table[32 * q : 32 * q + 4, :].bitcast(I32),
+                in_=x_scales[0, 4 * q : 4 * q + 4, :].bitcast(I32),
+            )
+
+        ident = keep.tile([P, P], F32, name="ident")
+        make_identity(nc, ident[:])
+
+        vel_rows = vel.rearrange("(p t) u -> t p u", t=TILES)
+        par_rows = par.rearrange("(p t) u -> t p u", t=TILES)
+        out_rows = out.rearrange("(p t) u -> t p u", t=TILES)
+        nc.sync.dma_start(out=vel_sb[0][:], in_=vel_rows[0])
+        nc.sync.dma_start(ent_sb[:], ent)
+        nc.sync.dma_start(offs_sb[:], offs)
+        nc.sync.dma_start(out=w_raw[:], in_=w1.rearrange("(p j) m -> p j m", j=PACK))
+        nc.sync.dma_start(out=x_table[:], in_=x_words[0].rearrange("p n r -> p (n r)").bitcast(I32))
+        nc.sync.dma_start(out=par_sb[0][:], in_=par_rows[0])
+        for t in (2, 1, 3):
+            nc.sync.dma_start(out=vel_sb[t][:], in_=vel_rows[t])
+            nc.sync.dma_start(out=par_sb[t][:], in_=par_rows[t])
+
+        x_scale = keep.tile([P, S], U8, name="x_scale", align_bytes=64)
+        nc.vector.tensor_copy(x_scale[:], xs_table[:].indirect(offs_sb[:]))
+
+        w_by_tile = w_raw[:].rearrange("p j (m t) -> p t m j", t=TILES)
+        grouped = []
+        for h in range(2):
+            pair = keep.tile([P, 2, P, PACK], BF16, name="grouped%d" % h, align_bytes=64)
+            if h == 0:
+                nc.vector.tensor_copy(out=pair[:], in_=w_by_tile[:, 0:2])
+            else:
+                nc.scalar.copy(out=pair[:], in_=w_by_tile[:, 2:4])
+            grouped.append(pair)
+
+        x_codes = keep.tile([P, S], U32, name="x_codes", align_bytes=64)
+        nc.vector.tensor_copy(x_codes[:], x_table[:].bitcast(U32).indirect(offs_sb[:]))
+
+        for t in range(TILES):
+            if t % 2 == 0:
+                w_codes = keep.tile([P, 2 * P], U32, name="w_codes", align_bytes=64)
+                w_scale = keep.tile([P, 2 * P], U8, name="w_scale", align_bytes=64)
+                nc.vector.quantize_mx(
+                    out=w_codes[:].bitcast(FP8X4),
+                    scales=w_scale[:],
+                    in_=grouped[t // 2][:].rearrange("p t m j -> p (t m j)"),
+                )
+            cols = slice((t % 2) * P, (t % 2 + 1) * P)
+            acc = psum.tile([P, S], F32, name="acc")
+            nc.tensor.matmul_mx(
+                out=acc[:],
+                lhsT=w_codes[:, cols].bitcast(FP8X4),
+                lhsT_scale=w_scale[:, cols],
+                rhs=x_codes[:].bitcast(FP8X4),
+                rhs_scale=x_scale[:],
+                start=True,
+                stop=True,
+            )
+            grad = keep.tile([P, S], F32, name="grad%d" % t)
+            nc.scalar.activation(out=grad[:], in_=acc[:], func=COPY, scale=GRAD_FACTOR)
+
+            both = keep.tile([P, S], F32, name="both%d" % t)
+            if t < 2:
+                vel_pick = keep.tile([P, S], F32, name="vel_pick%d" % t)
+                nc.vector.tensor_scalar(vel_pick[:], vel_sb[t][:].indirect(ent_sb[:]), VEL_FACTOR, 0.0, MULT, ADD)
+                nc.vector.tensor_tensor(both[:], par_sb[t][:].indirect(ent_sb[:]), vel_pick[:], ADD)
+            else:
+                summed = keep.tile([P, U], F32, name="summed%d" % t)
+                for h in range(2):
+                    half = slice(h * BANK, (h + 1) * BANK)
+                    scaled = work.tile([P, BANK], F32, name="scaled")
+                    nc.scalar.activation(out=scaled[:], in_=vel_sb[t][:, half], func=COPY, scale=VEL_FACTOR)
+                    turned = psum.tile([P, BANK], F32, name="turned", bufs=3)
+                    blocks = [slice(c * P, (c + 1) * P) for c in range(BANK // P)]
+                    for c, blk in enumerate(blocks):
+                        nc.tensor.matmul(turned[:, blk], scaled[:, blk], ident[:], start=(c == 0), stop=False, is_transpose=True)
+                    for c, blk in enumerate(blocks):
+                        nc.tensor.matmul(
+                            turned[:, blk], par_sb[t][:, half][:, blk], ident[:], start=False, stop=(c == len(blocks) - 1), is_transpose=True
+                        )
+                    turned_sb = work.tile([P, BANK], F32, name="turned_sb")
+                    nc.scalar.copy(out=turned_sb[:], in_=turned[:])
+                    back = psum.tile([P, BANK], F32, name="back", bufs=3)
+                    for c in range(BANK // P):
+                        blk = slice(c * P, (c + 1) * P)
+                        nc.tensor.transpose(back[:, blk], turned_sb[:, blk], ident[:])
+                    nc.scalar.copy(out=summed[:, half], in_=back[:])
+                nc.vector.tensor_copy(both[:], summed[:].indirect(ent_sb[:]))
+            nc.vector.tensor_tensor(par_sb[t][:].indirect(ent_sb[:]), both[:], grad[:], ADD)
+            nc.sync.dma_start(out=out_rows[t], in_=par_sb[t][:])

@@ -21,6 +21,7 @@ P = 128
 PACK = 4
 TILES = N // P
 BANK = 512
+SPLIT = 64
 VEL_FACTOR = 0.75 * 0.75
 GRAD_FACTOR = -(0.75 * 0.25 + 0.25)
 
@@ -53,42 +54,33 @@ def tile_picked_snag_none_p_kernel(tc, x_words, x_scales, w1, par, vel, offs, en
         vel_rows = vel.rearrange("(p t) u -> t p u", t=TILES)
         par_rows = par.rearrange("(p t) u -> t p u", t=TILES)
         out_rows = out.rearrange("(p t) u -> t p u", t=TILES)
-        nc.sync.dma_start(out=vel_sb[0][:], in_=vel_rows[0])
-        nc.sync.dma_start(ent_sb[:], ent)
         nc.sync.dma_start(offs_sb[:], offs)
         nc.sync.dma_start(out=w_raw[:], in_=w1.rearrange("(p j) m -> p j m", j=PACK))
         nc.sync.dma_start(out=x_table[:], in_=x_words[0].rearrange("p n r -> p (n r)").bitcast(I32))
-        nc.sync.dma_start(out=par_sb[0][:], in_=par_rows[0])
-        for t in (2, 1, 3):
+        nc.sync.dma_start(ent_sb[:], ent)
+        for t in (0, 2, 1, 3):
             nc.sync.dma_start(out=vel_sb[t][:], in_=vel_rows[t])
             nc.sync.dma_start(out=par_sb[t][:], in_=par_rows[t])
 
         x_scale = keep.tile([P, S], U8, name="x_scale", align_bytes=64)
         nc.vector.tensor_copy(x_scale[:], xs_table[:].indirect(offs_sb[:]))
 
-        w_by_tile = w_raw[:].rearrange("p j (m t) -> p t m j", t=TILES)
-        grouped = []
-        for h in range(2):
-            pair = keep.tile([P, 2, P, PACK], BF16, name="grouped%d" % h, align_bytes=64)
-            if h == 0:
-                nc.vector.tensor_copy(out=pair[:], in_=w_by_tile[:, 0:2])
-            else:
-                nc.scalar.copy(out=pair[:], in_=w_by_tile[:, 2:4])
-            grouped.append(pair)
+        grouped = keep.tile([P, TILES, P, PACK], BF16, name="grouped", align_bytes=64)
+        w_dst = grouped[:].rearrange("p t m j -> p m j t")
+        w_src = w_raw[:].rearrange("p j (m t) -> p m j t", t=TILES)
+        nc.vector.tensor_copy(out=w_dst[:, :SPLIT], in_=w_src[:, :SPLIT])
+        nc.scalar.copy(out=w_dst[:, SPLIT:], in_=w_src[:, SPLIT:])
+        w_codes = keep.tile([P, N], U32, name="w_codes", align_bytes=64)
+        w_scale = keep.tile([P, N], U8, name="w_scale", align_bytes=64)
+        nc.vector.quantize_mx(
+            out=w_codes[:].bitcast(FP8X4), scales=w_scale[:], in_=grouped[:].rearrange("p t m j -> p (t m j)")
+        )
 
         x_codes = keep.tile([P, S], U32, name="x_codes", align_bytes=64)
         nc.vector.tensor_copy(x_codes[:], x_table[:].bitcast(U32).indirect(offs_sb[:]))
 
-        for t in range(TILES):
-            if t % 2 == 0:
-                w_codes = keep.tile([P, 2 * P], U32, name="w_codes", align_bytes=64)
-                w_scale = keep.tile([P, 2 * P], U8, name="w_scale", align_bytes=64)
-                nc.vector.quantize_mx(
-                    out=w_codes[:].bitcast(FP8X4),
-                    scales=w_scale[:],
-                    in_=grouped[t // 2][:].rearrange("p t m j -> p (t m j)"),
-                )
-            cols = slice((t % 2) * P, (t % 2 + 1) * P)
+        def gradient(t):
+            cols = slice(t * P, (t + 1) * P)
             acc = psum.tile([P, S], F32, name="acc")
             nc.tensor.matmul_mx(
                 out=acc[:],
@@ -101,33 +93,41 @@ def tile_picked_snag_none_p_kernel(tc, x_words, x_scales, w1, par, vel, offs, en
             )
             grad = keep.tile([P, S], F32, name="grad%d" % t)
             nc.scalar.activation(out=grad[:], in_=acc[:], func=COPY, scale=GRAD_FACTOR)
+            return grad
 
+        def sum_by_transposes(t, half, summed):
+            blocks = [slice(c * P, (c + 1) * P) for c in range(BANK // P)]
+            scaled = work.tile([P, BANK], F32, name="scaled")
+            nc.scalar.activation(out=scaled[:], in_=vel_sb[t][:, half], func=COPY, scale=VEL_FACTOR)
+            turned = psum.tile([P, BANK], F32, name="turned", bufs=2)
+            for c, blk in enumerate(blocks):
+                nc.tensor.matmul(turned[:, blk], scaled[:, blk], ident[:], start=(c == 0), stop=False, is_transpose=True)
+            for c, blk in enumerate(blocks):
+                last = c == len(blocks) - 1
+                nc.tensor.matmul(turned[:, blk], par_sb[t][:, half][:, blk], ident[:], start=False, stop=last, is_transpose=True)
+            turned_sb = work.tile([P, BANK], F32, name="turned_sb")
+            nc.scalar.copy(out=turned_sb[:], in_=turned[:])
+            back = psum.tile([P, BANK], F32, name="back", bufs=3)
+            for blk in blocks:
+                nc.tensor.transpose(back[:, blk], turned_sb[:, blk], ident[:])
+            nc.scalar.copy(out=summed[:, half], in_=back[:])
+
+        halves = (slice(0, BANK), slice(BANK, U))
+        for t in range(TILES):
             both = keep.tile([P, S], F32, name="both%d" % t)
-            if t < 2:
-                vel_pick = keep.tile([P, S], F32, name="vel_pick%d" % t)
+            if t == 0:
+                grad = gradient(t)
+                vel_pick = keep.tile([P, S], F32, name="vel_pick")
                 nc.vector.tensor_scalar(vel_pick[:], vel_sb[t][:].indirect(ent_sb[:]), VEL_FACTOR, 0.0, MULT, ADD)
                 nc.vector.tensor_tensor(both[:], par_sb[t][:].indirect(ent_sb[:]), vel_pick[:], ADD)
             else:
                 summed = keep.tile([P, U], F32, name="summed%d" % t)
-                for h in range(2):
-                    half = slice(h * BANK, (h + 1) * BANK)
-                    scaled = work.tile([P, BANK], F32, name="scaled")
-                    nc.scalar.activation(out=scaled[:], in_=vel_sb[t][:, half], func=COPY, scale=VEL_FACTOR)
-                    turned = psum.tile([P, BANK], F32, name="turned", bufs=3)
-                    blocks = [slice(c * P, (c + 1) * P) for c in range(BANK // P)]
-                    for c, blk in enumerate(blocks):
-                        nc.tensor.matmul(turned[:, blk], scaled[:, blk], ident[:], start=(c == 0), stop=False, is_transpose=True)
-                    for c, blk in enumerate(blocks):
-                        nc.tensor.matmul(
-                            turned[:, blk], par_sb[t][:, half][:, blk], ident[:], start=False, stop=(c == len(blocks) - 1), is_transpose=True
-                        )
-                    turned_sb = work.tile([P, BANK], F32, name="turned_sb")
-                    nc.scalar.copy(out=turned_sb[:], in_=turned[:])
-                    back = psum.tile([P, BANK], F32, name="back", bufs=3)
-                    for c in range(BANK // P):
-                        blk = slice(c * P, (c + 1) * P)
-                        nc.tensor.transpose(back[:, blk], turned_sb[:, blk], ident[:])
-                    nc.scalar.copy(out=summed[:, half], in_=back[:])
+                if t == 1:
+                    nc.vector.scalar_tensor_tensor(summed[:], vel_sb[t][:], VEL_FACTOR, par_sb[t][:], MULT, ADD)
+                else:
+                    for half in halves:
+                        sum_by_transposes(t, half, summed)
+                grad = gradient(t)
                 nc.vector.tensor_copy(both[:], summed[:].indirect(ent_sb[:]))
             nc.vector.tensor_tensor(par_sb[t][:].indirect(ent_sb[:]), both[:], grad[:], ADD)
             nc.sync.dma_start(out=out_rows[t], in_=par_sb[t][:])

@@ -58,7 +58,7 @@ def tile_picked_snag_none_p_kernel(tc, x_words, x_scales, w1, par, vel, offs, en
         nc.sync.dma_start(out=w_raw[:], in_=w1.rearrange("(p j) m -> p j m", j=PACK))
         nc.sync.dma_start(out=x_table[:], in_=x_words[0].rearrange("p n r -> p (n r)").bitcast(I32))
         nc.sync.dma_start(ent_sb[:], ent)
-        for t in (0, 2, 1, 3):
+        for t in range(TILES):
             nc.sync.dma_start(out=vel_sb[t][:], in_=vel_rows[t])
             nc.sync.dma_start(out=par_sb[t][:], in_=par_rows[t])
 
@@ -91,9 +91,7 @@ def tile_picked_snag_none_p_kernel(tc, x_words, x_scales, w1, par, vel, offs, en
                 start=True,
                 stop=True,
             )
-            grad = keep.tile([P, S], F32, name="grad%d" % t)
-            nc.scalar.activation(out=grad[:], in_=acc[:], func=COPY, scale=GRAD_FACTOR)
-            return grad
+            return acc
 
         def sum_by_transposes(t, half, summed):
             blocks = [slice(c * P, (c + 1) * P) for c in range(BANK // P)]
@@ -113,21 +111,30 @@ def tile_picked_snag_none_p_kernel(tc, x_words, x_scales, w1, par, vel, offs, en
             nc.scalar.copy(out=summed[:, half], in_=back[:])
 
         halves = (slice(0, BANK), slice(BANK, U))
+        summed1 = keep.tile([P, U], F32, name="summed1")
+        vel_scaled = keep.tile([P, U], F32, name="vel_scaled")
         for t in range(TILES):
             both = keep.tile([P, S], F32, name="both%d" % t)
+            window = par_sb[t][:].indirect(ent_sb[:])
             if t == 0:
-                grad = gradient(t)
                 vel_pick = keep.tile([P, S], F32, name="vel_pick")
                 nc.vector.tensor_scalar(vel_pick[:], vel_sb[t][:].indirect(ent_sb[:]), VEL_FACTOR, 0.0, MULT, ADD)
-                nc.vector.tensor_tensor(both[:], par_sb[t][:].indirect(ent_sb[:]), vel_pick[:], ADD)
+                step = summed1[:, :S]
+                nc.vector.scalar_tensor_tensor(step, gradient(t)[:], GRAD_FACTOR, vel_pick[:], MULT, ADD)
+                nc.vector.tensor_tensor(both[:], window, step, ADD)
+                nc.vector.tensor_copy(window, both[:])
             else:
-                summed = keep.tile([P, U], F32, name="summed%d" % t)
                 if t == 1:
-                    nc.vector.scalar_tensor_tensor(summed[:], vel_sb[t][:], VEL_FACTOR, par_sb[t][:], MULT, ADD)
+                    summed = summed1
+                    nc.scalar.activation(out=vel_scaled[:], in_=vel_sb[t][:], func=COPY, scale=VEL_FACTOR)
+                    nc.gpsimd.tensor_tensor(summed[:], par_sb[t][:], vel_scaled[:], ADD)
+                    grad = keep.tile([P, S], F32, name="grad1")[:]
                 else:
+                    summed = keep.tile([P, U], F32, name="summed%d" % t)
                     for half in halves:
                         sum_by_transposes(t, half, summed)
-                grad = gradient(t)
+                    grad = vel_sb[1][:, halves[t - 2]]
+                nc.scalar.activation(out=grad, in_=gradient(t)[:], func=COPY, scale=GRAD_FACTOR)
                 nc.vector.tensor_copy(both[:], summed[:].indirect(ent_sb[:]))
-            nc.vector.tensor_tensor(par_sb[t][:].indirect(ent_sb[:]), both[:], grad[:], ADD)
+                nc.vector.tensor_tensor(window, both[:], grad, ADD)
             nc.sync.dma_start(out=out_rows[t], in_=par_sb[t][:])

@@ -22,6 +22,7 @@ PACK = 4
 TILES = N // P
 BANK = 512
 SPLIT = 64
+EARLY = 640
 VEL_FACTOR = 0.75 * 0.75
 GRAD_FACTOR = -(0.75 * 0.25 + 0.25)
 
@@ -58,7 +59,11 @@ def tile_picked_snag_none_p_kernel(tc, x_words, x_scales, w1, par, vel, offs, en
         nc.sync.dma_start(out=w_raw[:], in_=w1.rearrange("(p j) m -> p j m", j=PACK))
         nc.sync.dma_start(out=x_table[:], in_=x_words[0].rearrange("p n r -> p (n r)").bitcast(I32))
         nc.sync.dma_start(ent_sb[:], ent)
-        for t in range(TILES):
+        parts = (slice(0, EARLY), slice(EARLY, U))
+        for cols in parts:
+            nc.sync.dma_start(out=vel_sb[0][:, cols], in_=vel_rows[0][:, cols])
+            nc.sync.dma_start(out=par_sb[0][:, cols], in_=par_rows[0][:, cols])
+        for t in range(1, TILES):
             nc.sync.dma_start(out=vel_sb[t][:], in_=vel_rows[t])
             nc.sync.dma_start(out=par_sb[t][:], in_=par_rows[t])
 
@@ -117,11 +122,12 @@ def tile_picked_snag_none_p_kernel(tc, x_words, x_scales, w1, par, vel, offs, en
             both = keep.tile([P, S], F32, name="both%d" % t)
             window = par_sb[t][:].indirect(ent_sb[:])
             if t == 0:
-                vel_pick = keep.tile([P, S], F32, name="vel_pick")
-                nc.vector.tensor_scalar(vel_pick[:], vel_sb[t][:].indirect(ent_sb[:]), VEL_FACTOR, 0.0, MULT, ADD)
-                step = summed1[:, :S]
-                nc.vector.scalar_tensor_tensor(step, gradient(t)[:], GRAD_FACTOR, vel_pick[:], MULT, ADD)
-                nc.vector.tensor_tensor(both[:], window, step, ADD)
+                summed = keep.tile([P, U], F32, name="summed0")
+                for cols in parts:
+                    nc.vector.scalar_tensor_tensor(summed[:, cols], vel_sb[t][:, cols], VEL_FACTOR, par_sb[t][:, cols], MULT, ADD)
+                grad = summed1[:, :S]
+                nc.scalar.activation(out=grad, in_=gradient(t)[:], func=COPY, scale=GRAD_FACTOR)
+                nc.vector.tensor_tensor(both[:], summed[:].indirect(ent_sb[:]), grad, ADD)
                 nc.vector.tensor_copy(window, both[:])
             else:
                 if t == 1:

@@ -1,7 +1,6 @@
 from contextlib import ExitStack
 
 import concourse.mybir as mybir
-from concourse.masks import make_identity
 
 K, T, S, N, U = 512, 2048, 512, 512, 1024
 FLOPS = 2 * K * N * S
@@ -20,7 +19,6 @@ COPY = mybir.ActivationFunctionType.Copy
 P = 128
 PACK = 4
 TILES = N // P
-BANK = 512
 SPLIT = 64
 EARLY = 640
 VEL_FACTOR = 0.75 * 0.75
@@ -31,8 +29,7 @@ def tile_picked_snag_none_p_kernel(tc, x_words, x_scales, w1, par, vel, offs, en
     nc = tc.nc
     with ExitStack() as ctx:
         keep = ctx.enter_context(tc.tile_pool(name="keep", bufs=1))
-        psum = ctx.enter_context(tc.psum_pool(name="psum", bufs=2))
-        work = ctx.enter_context(tc.tile_pool(name="work", bufs=2))
+        psum = ctx.enter_context(tc.psum_pool(name="psum", bufs=TILES))
 
         offs_sb = keep.tile([P, S // 16], U16, name="offs_sb")
         ent_sb = keep.tile([P, S // 16], U16, name="ent_sb")
@@ -48,9 +45,6 @@ def tile_picked_snag_none_p_kernel(tc, x_words, x_scales, w1, par, vel, offs, en
                 out=xs_table[32 * q : 32 * q + 4, :].bitcast(I32),
                 in_=x_scales[0, 4 * q : 4 * q + 4, :].bitcast(I32),
             )
-
-        ident = keep.tile([P, P], F32, name="ident")
-        make_identity(nc, ident[:])
 
         vel_rows = vel.rearrange("(p t) u -> t p u", t=TILES)
         par_rows = par.rearrange("(p t) u -> t p u", t=TILES)
@@ -98,49 +92,18 @@ def tile_picked_snag_none_p_kernel(tc, x_words, x_scales, w1, par, vel, offs, en
             )
             return acc
 
-        def sum_by_transposes(t, half, summed):
-            blocks = [slice(c * P, (c + 1) * P) for c in range(BANK // P)]
-            scaled = work.tile([P, BANK], F32, name="scaled")
-            nc.scalar.activation(out=scaled[:], in_=vel_sb[t][:, half], func=COPY, scale=VEL_FACTOR)
-            turned = psum.tile([P, BANK], F32, name="turned", bufs=2)
-            for c, blk in enumerate(blocks):
-                nc.tensor.matmul(turned[:, blk], scaled[:, blk], ident[:], start=(c == 0), stop=False, is_transpose=True)
-            for c, blk in enumerate(blocks):
-                last = c == len(blocks) - 1
-                nc.tensor.matmul(turned[:, blk], par_sb[t][:, half][:, blk], ident[:], start=False, stop=last, is_transpose=True)
-            turned_sb = work.tile([P, BANK], F32, name="turned_sb")
-            nc.scalar.copy(out=turned_sb[:], in_=turned[:])
-            back = psum.tile([P, BANK], F32, name="back", bufs=3)
-            for blk in blocks:
-                nc.tensor.transpose(back[:, blk], turned_sb[:, blk], ident[:])
-            nc.scalar.copy(out=summed[:, half], in_=back[:])
-
-        halves = (slice(0, BANK), slice(BANK, U))
-        summed1 = keep.tile([P, U], F32, name="summed1")
-        vel_scaled = keep.tile([P, U], F32, name="vel_scaled")
+        summed = [keep.tile([P, U], F32, name="summed0")] + vel_sb[:-1]
+        for cols in parts:
+            nc.vector.scalar_tensor_tensor(summed[0][:, cols], vel_sb[0][:, cols], VEL_FACTOR, par_sb[0][:, cols], MULT, ADD)
         for t in range(TILES):
-            both = keep.tile([P, S], F32, name="both%d" % t)
-            window = par_sb[t][:].indirect(ent_sb[:])
-            if t == 0:
-                summed = keep.tile([P, U], F32, name="summed0")
-                for cols in parts:
-                    nc.vector.scalar_tensor_tensor(summed[:, cols], vel_sb[t][:, cols], VEL_FACTOR, par_sb[t][:, cols], MULT, ADD)
-                grad = summed1[:, :S]
-                nc.scalar.activation(out=grad, in_=gradient(t)[:], func=COPY, scale=GRAD_FACTOR)
-                nc.vector.tensor_tensor(both[:], summed[:].indirect(ent_sb[:]), grad, ADD)
-                nc.vector.tensor_copy(window, both[:])
-            else:
-                if t == 1:
-                    summed = summed1
-                    nc.scalar.activation(out=vel_scaled[:], in_=vel_sb[t][:], func=COPY, scale=VEL_FACTOR)
-                    nc.gpsimd.tensor_tensor(summed[:], par_sb[t][:], vel_scaled[:], ADD)
-                    grad = keep.tile([P, S], F32, name="grad1")[:]
-                else:
-                    summed = keep.tile([P, U], F32, name="summed%d" % t)
-                    for half in halves:
-                        sum_by_transposes(t, half, summed)
-                    grad = vel_sb[1][:, halves[t - 2]]
-                nc.scalar.activation(out=grad, in_=gradient(t)[:], func=COPY, scale=GRAD_FACTOR)
-                nc.vector.tensor_copy(both[:], summed[:].indirect(ent_sb[:]))
-                nc.vector.tensor_tensor(window, both[:], grad, ADD)
+            if t > 0:
+                nc.gpsimd.tensor_tensor(summed[t][:], par_sb[t][:], vel_scaled[:], ADD)
+            grad = vel_sb[t][:, :S]
+            nc.scalar.activation(out=grad, in_=gradient(t)[:], func=COPY, scale=GRAD_FACTOR)
+            if t + 1 < TILES:
+                vel_scaled = keep.tile([P, U], F32, name="vel_scaled%d" % t)
+                nc.scalar.activation(out=vel_scaled[:], in_=vel_sb[t + 1][:], func=COPY, scale=VEL_FACTOR)
+            moved = keep.tile([P, S], F32, name="moved%d" % t)
+            nc.vector.tensor_tensor(moved[:], summed[t][:].indirect(ent_sb[:]), grad, ADD)
+            nc.vector.tensor_copy(par_sb[t][:].indirect(ent_sb[:]), moved[:])
             nc.sync.dma_start(out=out_rows[t], in_=par_sb[t][:])

@@ -1,6 +1,7 @@
 from contextlib import ExitStack
 
 import concourse.mybir as mybir
+from concourse.masks import make_identity
 
 K, T, S, N, U = 512, 2048, 512, 512, 1024
 FLOPS = 2 * K * N * S
@@ -45,6 +46,9 @@ def tile_picked_snag_none_p_kernel(tc, x_words, x_scales, w1, par, vel, offs, en
                 out=xs_table[32 * q : 32 * q + 4, :].bitcast(I32),
                 in_=x_scales[0, 4 * q : 4 * q + 4, :].bitcast(I32),
             )
+
+        ident = keep.tile([P, P], F32, name="ident")
+        make_identity(nc, ident[:])
 
         vel_rows = vel.rearrange("(p t) u -> t p u", t=TILES)
         par_rows = par.rearrange("(p t) u -> t p u", t=TILES)
@@ -92,18 +96,56 @@ def tile_picked_snag_none_p_kernel(tc, x_words, x_scales, w1, par, vel, offs, en
             )
             return acc
 
-        summed = [keep.tile([P, U], F32, name="summed0")] + vel_sb[:-1]
+        halves = (slice(0, S), slice(S, U))
+        blocks = [slice(c * P, (c + 1) * P) for c in range(S // P)]
+        summed = [keep.tile([P, U], F32, name="summed%d" % t) for t in range(TILES - 1)] + [vel_sb[1]]
+        scaled = {t: keep.tile([P, U], F32, name="scaled%d" % t) for t in range(1, TILES)}
+
+        def scale_vel(t, cols):
+            nc.scalar.activation(out=scaled[t][:, cols], in_=vel_sb[t][:, cols], func=COPY, scale=VEL_FACTOR)
+
+        def add_rows(t):
+            nc.gpsimd.tensor_tensor(summed[t][:], par_sb[t][:], scaled[t][:], ADD)
+
+        def add_by_transposes(t):
+            for half in halves:
+                turned = psum.tile([P, S], F32, name="turned", bufs=2)
+                for c, blk in enumerate(blocks):
+                    nc.tensor.matmul(turned[:, blk], scaled[t][:, half][:, blk], ident[:], start=(c == 0), stop=False, is_transpose=True)
+                for c, blk in enumerate(blocks):
+                    last = c == len(blocks) - 1
+                    nc.tensor.matmul(turned[:, blk], par_sb[t][:, half][:, blk], ident[:], start=False, stop=last, is_transpose=True)
+                nc.scalar.copy(out=scaled[t][:, half], in_=turned[:])
+            for half in halves:
+                back = psum.tile([P, S], F32, name="back", bufs=2)
+                for blk in blocks:
+                    nc.tensor.transpose(back[:, blk], scaled[t][:, half][:, blk], ident[:])
+                nc.scalar.copy(out=summed[t][:, half], in_=back[:])
+
+        def gather(t, grad, moved):
+            nc.scalar.activation(out=grad, in_=gradient(t)[:], func=COPY, scale=GRAD_FACTOR)
+            nc.vector.tensor_tensor(moved, summed[t][:].indirect(ent_sb[:]), grad, ADD)
+
+        def scatter(t, moved):
+            nc.vector.tensor_copy(par_sb[t][:].indirect(ent_sb[:]), moved)
+            nc.sync.dma_start(out=out_rows[t], in_=par_sb[t][:])
+
         for cols in parts:
             nc.vector.scalar_tensor_tensor(summed[0][:, cols], vel_sb[0][:, cols], VEL_FACTOR, par_sb[0][:, cols], MULT, ADD)
-        for t in range(TILES):
-            if t > 0:
-                nc.gpsimd.tensor_tensor(summed[t][:], par_sb[t][:], vel_scaled[:], ADD)
-            grad = vel_sb[t][:, :S]
-            nc.scalar.activation(out=grad, in_=gradient(t)[:], func=COPY, scale=GRAD_FACTOR)
-            if t + 1 < TILES:
-                vel_scaled = keep.tile([P, U], F32, name="vel_scaled%d" % t)
-                nc.scalar.activation(out=vel_scaled[:], in_=vel_sb[t + 1][:], func=COPY, scale=VEL_FACTOR)
-            moved = keep.tile([P, S], F32, name="moved%d" % t)
-            nc.vector.tensor_tensor(moved[:], summed[t][:].indirect(ent_sb[:]), grad, ADD)
-            nc.vector.tensor_copy(par_sb[t][:].indirect(ent_sb[:]), moved[:])
-            nc.sync.dma_start(out=out_rows[t], in_=par_sb[t][:])
+        own = {t: keep.tile([P, S], F32, name="moved%d" % t) for t in (0, 1, 3)}
+        moved = [own[0][:], own[1][:], scaled[3][:, :S], own[3][:]]
+        gather(0, summed[1][:, :S], moved[0])
+        scatter(0, moved[0])
+        scale_vel(1, slice(0, U))
+        add_rows(1)
+        gather(1, vel_sb[1][:, :S], moved[1])
+        scatter(1, moved[1])
+        scale_vel(3, slice(0, U))
+        add_rows(3)
+        for half in halves:
+            scale_vel(2, half)
+        add_by_transposes(2)
+        gather(2, vel_sb[2][:, halves[1]], moved[2])
+        gather(3, vel_sb[3][:, :S], moved[3])
+        scatter(2, moved[2])
+        scatter(3, moved[3])

@@ -61,9 +61,10 @@ def tile_picked_snag_none_p_kernel(tc, x_words, x_scales, w1, par, vel, offs, en
         for cols in parts:
             nc.sync.dma_start(out=vel_sb[0][:, cols], in_=vel_rows[0][:, cols])
             nc.sync.dma_start(out=par_sb[0][:, cols], in_=par_rows[0][:, cols])
-        for t in range(1, TILES):
-            nc.sync.dma_start(out=vel_sb[t][:], in_=vel_rows[t])
-            nc.sync.dma_start(out=par_sb[t][:], in_=par_rows[t])
+        halves = (slice(0, S), slice(S, U))
+        for t, cols in ((1, slice(0, U)), (2, slice(0, U)), (3, halves[0]), (3, halves[1])):
+            nc.sync.dma_start(out=vel_sb[t][:, cols], in_=vel_rows[t][:, cols])
+            nc.sync.dma_start(out=par_sb[t][:, cols], in_=par_rows[t][:, cols])
 
         x_scale = keep.tile([P, S], U8, name="x_scale", align_bytes=64)
         nc.vector.tensor_copy(x_scale[:], xs_table[:].indirect(offs_sb[:]))
@@ -96,7 +97,6 @@ def tile_picked_snag_none_p_kernel(tc, x_words, x_scales, w1, par, vel, offs, en
             )
             return acc
 
-        halves = (slice(0, S), slice(S, U))
         blocks = [slice(c * P, (c + 1) * P) for c in range(S // P)]
         summed = [keep.tile([P, U], F32, name="summed%d" % t) for t in range(TILES - 1)] + [vel_sb[1]]
         scaled = {t: keep.tile([P, U], F32, name="scaled%d" % t) for t in range(1, TILES)}
@@ -104,8 +104,8 @@ def tile_picked_snag_none_p_kernel(tc, x_words, x_scales, w1, par, vel, offs, en
         def scale_vel(t, cols):
             nc.scalar.activation(out=scaled[t][:, cols], in_=vel_sb[t][:, cols], func=COPY, scale=VEL_FACTOR)
 
-        def add_rows(t):
-            nc.gpsimd.tensor_tensor(summed[t][:], par_sb[t][:], scaled[t][:], ADD)
+        def add_rows(t, cols):
+            nc.gpsimd.tensor_tensor(summed[t][:, cols], par_sb[t][:, cols], scaled[t][:, cols], ADD)
 
         def add_by_transposes(t):
             for half in halves:
@@ -133,19 +133,20 @@ def tile_picked_snag_none_p_kernel(tc, x_words, x_scales, w1, par, vel, offs, en
         for cols in parts:
             nc.vector.scalar_tensor_tensor(summed[0][:, cols], vel_sb[0][:, cols], VEL_FACTOR, par_sb[0][:, cols], MULT, ADD)
         own = {t: keep.tile([P, S], F32, name="moved%d" % t) for t in (0, 1, 3)}
-        moved = [own[0][:], own[1][:], scaled[3][:, :S], own[3][:]]
+        moved = [own[0][:], own[1][:], scaled[3][:, halves[1]], own[3][:]]
         gather(0, summed[1][:, :S], moved[0])
         scatter(0, moved[0])
         scale_vel(1, slice(0, U))
-        add_rows(1)
+        add_rows(1, slice(0, U))
         gather(1, vel_sb[1][:, :S], moved[1])
         scatter(1, moved[1])
-        scale_vel(3, slice(0, U))
-        add_rows(3)
+        for half in halves:
+            scale_vel(3, half)
+            add_rows(3, half)
         for half in halves:
             scale_vel(2, half)
         add_by_transposes(2)
         gather(2, vel_sb[2][:, halves[1]], moved[2])
-        gather(3, vel_sb[3][:, :S], moved[3])
+        gather(3, vel_sb[3][:, halves[1]], moved[3])
         scatter(2, moved[2])
         scatter(3, moved[3])

@@ -21,7 +21,7 @@ P = 128
 PACK = 4
 TILES = N // P
 SPLIT = 64
-EARLY = 640
+EARLY = 704
 VEL_FACTOR = 0.75 * 0.75
 GRAD_FACTOR = -(0.75 * 0.25 + 0.25)
 
@@ -56,11 +56,11 @@ def tile_picked_snag_none_p_kernel(tc, x_words, x_scales, w1, par, vel, offs, en
         nc.sync.dma_start(offs_sb[:], offs)
         nc.sync.dma_start(out=w_raw[:], in_=w1.rearrange("(p j) m -> p j m", j=PACK))
         nc.sync.dma_start(out=x_table[:], in_=x_words[0].rearrange("p n r -> p (n r)").bitcast(I32))
-        nc.sync.dma_start(ent_sb[:], ent)
         parts = (slice(0, EARLY), slice(EARLY, U))
         for cols in parts:
             nc.sync.dma_start(out=vel_sb[0][:, cols], in_=vel_rows[0][:, cols])
             nc.sync.dma_start(out=par_sb[0][:, cols], in_=par_rows[0][:, cols])
+        nc.sync.dma_start(ent_sb[:], ent)
         halves = (slice(0, S), slice(S, U))
         for t, cols in ((1, slice(0, U)), (2, slice(0, U)), (3, halves[0]), (3, halves[1])):
             nc.sync.dma_start(out=vel_sb[t][:, cols], in_=vel_rows[t][:, cols])
@@ -81,17 +81,19 @@ def tile_picked_snag_none_p_kernel(tc, x_words, x_scales, w1, par, vel, offs, en
         )
 
         x_codes = keep.tile([P, S], U32, name="x_codes", align_bytes=64)
-        nc.vector.tensor_copy(x_codes[:], x_table[:].bitcast(U32).indirect(offs_sb[:]))
+        picks = (slice(0, S // 2), slice(S // 2, S))
+        for pick in picks:
+            nc.vector.tensor_copy(x_codes[:, pick], x_table[:].bitcast(U32).indirect(offs_sb[:, pick.start // 16 : pick.stop // 16]))
 
-        def gradient(t):
+        def gradient(t, pick):
             cols = slice(t * P, (t + 1) * P)
-            acc = psum.tile([P, S], F32, name="acc")
+            acc = psum.tile([P, pick.stop - pick.start], F32, name="acc")
             nc.tensor.matmul_mx(
                 out=acc[:],
                 lhsT=w_codes[:, cols].bitcast(FP8X4),
                 lhsT_scale=w_scale[:, cols],
-                rhs=x_codes[:].bitcast(FP8X4),
-                rhs_scale=x_scale[:],
+                rhs=x_codes[:, pick].bitcast(FP8X4),
+                rhs_scale=x_scale[:, pick],
                 start=True,
                 stop=True,
             )
@@ -123,7 +125,8 @@ def tile_picked_snag_none_p_kernel(tc, x_words, x_scales, w1, par, vel, offs, en
                 nc.scalar.copy(out=summed[t][:, half], in_=back[:])
 
         def gather(t, grad, moved):
-            nc.scalar.activation(out=grad, in_=gradient(t)[:], func=COPY, scale=GRAD_FACTOR)
+            for pick in picks if t == 0 else (slice(0, S),):
+                nc.scalar.activation(out=grad[:, pick], in_=gradient(t, pick)[:], func=COPY, scale=GRAD_FACTOR)
             nc.vector.tensor_tensor(moved, summed[t][:].indirect(ent_sb[:]), grad, ADD)
 
         def scatter(t, moved):

@@ -1,7 +1,6 @@
 from contextlib import ExitStack
 
 import concourse.mybir as mybir
-from concourse.masks import make_identity
 
 K, T, S, N, U = 512, 2048, 512, 512, 1024
 FLOPS = 2 * K * N * S
@@ -21,7 +20,6 @@ P = 128
 PACK = 4
 TILES = N // P
 SPLIT = 64
-EARLY = 704
 VEL_FACTOR = 0.75 * 0.75
 GRAD_FACTOR = -(0.75 * 0.25 + 0.25)
 
@@ -30,7 +28,7 @@ def tile_picked_snag_none_p_kernel(tc, x_words, x_scales, w1, par, vel, offs, en
     nc = tc.nc
     with ExitStack() as ctx:
         keep = ctx.enter_context(tc.tile_pool(name="keep", bufs=1))
-        psum = ctx.enter_context(tc.psum_pool(name="psum", bufs=TILES))
+        psum = ctx.enter_context(tc.psum_pool(name="psum", bufs=1))
 
         offs_sb = keep.tile([P, S // 16], U16, name="offs_sb")
         ent_sb = keep.tile([P, S // 16], U16, name="ent_sb")
@@ -47,24 +45,18 @@ def tile_picked_snag_none_p_kernel(tc, x_words, x_scales, w1, par, vel, offs, en
                 in_=x_scales[0, 4 * q : 4 * q + 4, :].bitcast(I32),
             )
 
-        ident = keep.tile([P, P], F32, name="ident")
-        make_identity(nc, ident[:])
-
         vel_rows = vel.rearrange("(p t) u -> t p u", t=TILES)
         par_rows = par.rearrange("(p t) u -> t p u", t=TILES)
         out_rows = out.rearrange("(p t) u -> t p u", t=TILES)
         nc.sync.dma_start(offs_sb[:], offs)
         nc.sync.dma_start(out=w_raw[:], in_=w1.rearrange("(p j) m -> p j m", j=PACK))
         nc.sync.dma_start(out=x_table[:], in_=x_words[0].rearrange("p n r -> p (n r)").bitcast(I32))
-        parts = (slice(0, EARLY), slice(EARLY, U))
-        for cols in parts:
-            nc.sync.dma_start(out=vel_sb[0][:, cols], in_=vel_rows[0][:, cols])
-            nc.sync.dma_start(out=par_sb[0][:, cols], in_=par_rows[0][:, cols])
+        nc.sync.dma_start(out=vel_sb[0][:], in_=vel_rows[0])
         nc.sync.dma_start(ent_sb[:], ent)
-        halves = (slice(0, S), slice(S, U))
-        for t, cols in ((1, slice(0, U)), (2, slice(0, U)), (3, halves[0]), (3, halves[1])):
-            nc.sync.dma_start(out=vel_sb[t][:, cols], in_=vel_rows[t][:, cols])
-            nc.sync.dma_start(out=par_sb[t][:, cols], in_=par_rows[t][:, cols])
+        nc.sync.dma_start(out=par_sb[0][:], in_=par_rows[0])
+        for t in range(1, TILES):
+            nc.sync.dma_start(out=par_sb[t][:], in_=par_rows[t])
+            nc.sync.dma_start(out=vel_sb[t][:], in_=vel_rows[t])
 
         x_scale = keep.tile([P, S], U8, name="x_scale", align_bytes=64)
         nc.vector.tensor_copy(x_scale[:], xs_table[:].indirect(offs_sb[:]))
@@ -80,14 +72,18 @@ def tile_picked_snag_none_p_kernel(tc, x_words, x_scales, w1, par, vel, offs, en
             out=w_codes[:].bitcast(FP8X4), scales=w_scale[:], in_=grouped[:].rearrange("p t m j -> p (t m j)")
         )
 
-        x_codes = keep.tile([P, S], U32, name="x_codes", align_bytes=64)
-        picks = (slice(0, S // 2), slice(S // 2, S))
-        for pick in picks:
-            nc.vector.tensor_copy(x_codes[:, pick], x_table[:].bitcast(U32).indirect(offs_sb[:, pick.start // 16 : pick.stop // 16]))
+        halves = (slice(0, S // 2), slice(S // 2, S))
 
-        def gradient(t, pick):
+        def entries(tile, pick):
+            return tile[:, pick.start // 16 : pick.stop // 16]
+
+        x_codes = keep.tile([P, S], U32, name="x_codes", align_bytes=64)
+        for pick in halves:
+            nc.vector.tensor_copy(x_codes[:, pick], x_table[:].bitcast(U32).indirect(entries(offs_sb, pick)))
+
+        def product(t, pick, name):
             cols = slice(t * P, (t + 1) * P)
-            acc = psum.tile([P, pick.stop - pick.start], F32, name="acc")
+            acc = psum.tile([P, pick.stop - pick.start], F32, name=name)
             nc.tensor.matmul_mx(
                 out=acc[:],
                 lhsT=w_codes[:, cols].bitcast(FP8X4),
@@ -99,57 +95,47 @@ def tile_picked_snag_none_p_kernel(tc, x_words, x_scales, w1, par, vel, offs, en
             )
             return acc
 
-        blocks = [slice(c * P, (c + 1) * P) for c in range(S // P)]
-        summed = [keep.tile([P, U], F32, name="summed%d" % t) for t in range(TILES - 1)] + [vel_sb[1]]
-        scaled = {t: keep.tile([P, U], F32, name="scaled%d" % t) for t in range(1, TILES)}
+        def fetch(dst, table, pick, factor):
+            nc.scalar.activation(out=dst, in_=table[:].indirect(entries(ent_sb, pick)), func=COPY, scale=factor)
 
-        def scale_vel(t, cols):
-            nc.scalar.activation(out=scaled[t][:, cols], in_=vel_sb[t][:, cols], func=COPY, scale=VEL_FACTOR)
+        def scatter(t, pick, values):
+            nc.vector.tensor_copy(par_sb[t][:].indirect(entries(ent_sb, pick)), values)
 
-        def add_rows(t, cols):
-            nc.gpsimd.tensor_tensor(summed[t][:, cols], par_sb[t][:, cols], scaled[t][:, cols], ADD)
+        gv = [keep.tile([P, S], F32, name="gv%d" % t) for t in range(TILES)]
+        gp = [keep.tile([P, S], F32, name="gp%d" % t) for t in range(TILES)]
+        step = [keep.tile([P, S], F32, name="step%d" % t) for t in range(TILES)]
+        shared = keep.tile([P, S + S // 2], F32, name="shared")
+        step0a = shared[:, S // 4 : 3 * S // 4]
+        step0b = shared[:, : S // 2]
+        grad = [None, shared[:, S // 2 :], vel_sb[1][:, :S], vel_sb[2][:, :S]]
+        a, b = halves
+        whole = (slice(0, S),)
 
-        def add_by_transposes(t):
-            for half in halves:
-                turned = psum.tile([P, S], F32, name="turned", bufs=2)
-                for c, blk in enumerate(blocks):
-                    nc.tensor.matmul(turned[:, blk], scaled[t][:, half][:, blk], ident[:], start=(c == 0), stop=False, is_transpose=True)
-                for c, blk in enumerate(blocks):
-                    last = c == len(blocks) - 1
-                    nc.tensor.matmul(turned[:, blk], par_sb[t][:, half][:, blk], ident[:], start=False, stop=last, is_transpose=True)
-                nc.scalar.copy(out=scaled[t][:, half], in_=turned[:])
-            for half in halves:
-                back = psum.tile([P, S], F32, name="back", bufs=2)
-                for blk in blocks:
-                    nc.tensor.transpose(back[:, blk], scaled[t][:, half][:, blk], ident[:])
-                nc.scalar.copy(out=summed[t][:, half], in_=back[:])
+        acc_a = product(0, a, "acc0a")
+        acc_b = product(0, b, "acc0b")
+        fetch(gv[0][:, a], vel_sb[0], a, VEL_FACTOR)
+        fetch(gv[0][:, b], vel_sb[0], b, VEL_FACTOR)
+        nc.vector.scalar_tensor_tensor(step0a, acc_a[:], GRAD_FACTOR, gv[0][:, a], MULT, ADD)
+        nc.vector.tensor_tensor(gp[0][:, a], par_sb[0][:].indirect(entries(ent_sb, a)), step0a, ADD)
+        fetch(gp[0][:, b], par_sb[0], b, 1.0)
+        nc.vector.scalar_tensor_tensor(step0b, acc_b[:], GRAD_FACTOR, gv[0][:, b], MULT, ADD)
+        scatter(0, a, gp[0][:, a])
+        nc.gpsimd.tensor_tensor(step[0][:, b], step0b, gp[0][:, b], ADD)
+        scatter(0, b, step[0][:, b])
+        nc.sync.dma_start(out=out_rows[0], in_=par_sb[0][:])
 
-        def gather(t, grad, moved):
-            for pick in picks if t == 0 else (slice(0, S),):
-                nc.scalar.activation(out=grad[:, pick], in_=gradient(t, pick)[:], func=COPY, scale=GRAD_FACTOR)
-            nc.vector.tensor_tensor(moved, summed[t][:].indirect(ent_sb[:]), grad, ADD)
-
-        def scatter(t, moved):
-            nc.vector.tensor_copy(par_sb[t][:].indirect(ent_sb[:]), moved)
+        for t in range(1, TILES):
+            last = t == TILES - 1
+            acc = product(t, slice(0, S), "acc%d" % t)
+            nc.scalar.activation(out=grad[t], in_=acc[:], func=COPY, scale=GRAD_FACTOR)
+            for pick in halves if t == 1 else whole:
+                fetch(gp[t][:, pick], par_sb[t], pick, 1.0)
+                nc.gpsimd.tensor_tensor(step[t][:, pick], gp[t][:, pick], grad[t][:, pick], ADD)
+            for pick in whole if last else halves:
+                fetch(gv[t][:, pick], vel_sb[t], pick, VEL_FACTOR)
+                if last:
+                    nc.vector.tensor_tensor(par_sb[t][:].indirect(ent_sb[:]), step[t][:], gv[t][:], ADD)
+                else:
+                    nc.gpsimd.tensor_tensor(gp[t][:, pick], step[t][:, pick], gv[t][:, pick], ADD)
+                    scatter(t, pick, gp[t][:, pick])
             nc.sync.dma_start(out=out_rows[t], in_=par_sb[t][:])
-
-        for cols in parts:
-            nc.vector.scalar_tensor_tensor(summed[0][:, cols], vel_sb[0][:, cols], VEL_FACTOR, par_sb[0][:, cols], MULT, ADD)
-        own = {t: keep.tile([P, S], F32, name="moved%d" % t) for t in (0, 1, 3)}
-        moved = [own[0][:], own[1][:], scaled[3][:, halves[1]], own[3][:]]
-        gather(0, summed[1][:, :S], moved[0])
-        scatter(0, moved[0])
-        scale_vel(1, slice(0, U))
-        add_rows(1, slice(0, U))
-        gather(1, vel_sb[1][:, :S], moved[1])
-        scatter(1, moved[1])
-        for half in halves:
-            scale_vel(3, half)
-            add_rows(3, half)
-        for half in halves:
-            scale_vel(2, half)
-        add_by_transposes(2)
-        gather(2, vel_sb[2][:, halves[1]], moved[2])
-        gather(3, vel_sb[3][:, halves[1]], moved[3])
-        scatter(2, moved[2])
-        scatter(3, moved[3])

@@ -55,8 +55,8 @@ def tile_picked_snag_none_p_kernel(tc, x_words, x_scales, w1, par, vel, offs, en
         nc.sync.dma_start(ent_sb[:], ent)
         nc.sync.dma_start(out=par_sb[0][:], in_=par_rows[0])
         for t in range(1, TILES):
-            nc.sync.dma_start(out=par_sb[t][:], in_=par_rows[t])
             nc.sync.dma_start(out=vel_sb[t][:], in_=vel_rows[t])
+            nc.sync.dma_start(out=par_sb[t][:], in_=par_rows[t])
 
         x_scale = keep.tile([P, S], U8, name="x_scale", align_bytes=64)
         nc.vector.tensor_copy(x_scale[:], xs_table[:].indirect(offs_sb[:]))
@@ -103,39 +103,43 @@ def tile_picked_snag_none_p_kernel(tc, x_words, x_scales, w1, par, vel, offs, en
 
         gv = [keep.tile([P, S], F32, name="gv%d" % t) for t in range(TILES)]
         gp = [keep.tile([P, S], F32, name="gp%d" % t) for t in range(TILES)]
-        step = [keep.tile([P, S], F32, name="step%d" % t) for t in range(TILES)]
-        shared = keep.tile([P, S + S // 2], F32, name="shared")
-        step0a = shared[:, S // 4 : 3 * S // 4]
-        step0b = shared[:, : S // 2]
-        grad = [None, shared[:, S // 2 :], vel_sb[1][:, :S], vel_sb[2][:, :S]]
+        step = keep.tile([P, S], F32, name="step")
+        step0 = keep.tile([P, S], F32, name="step0")
         a, b = halves
-        whole = (slice(0, S),)
+        whole = slice(0, S)
 
         acc_a = product(0, a, "acc0a")
         acc_b = product(0, b, "acc0b")
         fetch(gv[0][:, a], vel_sb[0], a, VEL_FACTOR)
         fetch(gv[0][:, b], vel_sb[0], b, VEL_FACTOR)
-        nc.vector.scalar_tensor_tensor(step0a, acc_a[:], GRAD_FACTOR, gv[0][:, a], MULT, ADD)
-        nc.vector.tensor_tensor(gp[0][:, a], par_sb[0][:].indirect(entries(ent_sb, a)), step0a, ADD)
+        nc.vector.scalar_tensor_tensor(step0[:, a], acc_a[:], GRAD_FACTOR, gv[0][:, a], MULT, ADD)
+        nc.vector.tensor_tensor(gp[0][:, a], par_sb[0][:].indirect(entries(ent_sb, a)), step0[:, a], ADD)
         fetch(gp[0][:, b], par_sb[0], b, 1.0)
-        nc.vector.scalar_tensor_tensor(step0b, acc_b[:], GRAD_FACTOR, gv[0][:, b], MULT, ADD)
+        nc.vector.scalar_tensor_tensor(step0[:, b], acc_b[:], GRAD_FACTOR, gp[0][:, b], MULT, ADD)
         scatter(0, a, gp[0][:, a])
-        nc.gpsimd.tensor_tensor(step[0][:, b], step0b, gp[0][:, b], ADD)
-        scatter(0, b, step[0][:, b])
-        nc.sync.dma_start(out=out_rows[0], in_=par_sb[0][:])
 
-        for t in range(1, TILES):
-            last = t == TILES - 1
-            acc = product(t, slice(0, S), "acc%d" % t)
-            nc.scalar.activation(out=grad[t], in_=acc[:], func=COPY, scale=GRAD_FACTOR)
-            for pick in halves if t == 1 else whole:
-                fetch(gp[t][:, pick], par_sb[t], pick, 1.0)
-                nc.gpsimd.tensor_tensor(step[t][:, pick], gp[t][:, pick], grad[t][:, pick], ADD)
-            for pick in whole if last else halves:
-                fetch(gv[t][:, pick], vel_sb[t], pick, VEL_FACTOR)
-                if last:
-                    nc.vector.tensor_tensor(par_sb[t][:].indirect(ent_sb[:]), step[t][:], gv[t][:], ADD)
-                else:
-                    nc.gpsimd.tensor_tensor(gp[t][:, pick], step[t][:, pick], gv[t][:, pick], ADD)
-                    scatter(t, pick, gp[t][:, pick])
+        acc = product(1, whole, "acc1")
+        fetch(gv[1][:], vel_sb[1], whole, VEL_FACTOR)
+        nc.vector.scalar_tensor_tensor(step[:], acc[:], GRAD_FACTOR, gv[1][:], MULT, ADD)
+        nc.gpsimd.tensor_tensor(vel_sb[1][:, a], step0[:, b], gv[0][:, b], ADD)
+        scatter(0, b, vel_sb[1][:, a])
+        nc.sync.dma_start(out=out_rows[0], in_=par_sb[0][:])
+        fetch(gp[1][:], par_sb[1], whole, 1.0)
+        nc.gpsimd.tensor_tensor(gv[1][:], step[:], gp[1][:], ADD)
+        scatter(1, whole, gv[1][:])
+        nc.sync.dma_start(out=out_rows[1], in_=par_sb[1][:])
+
+        last = TILES - 1
+        for t in range(2, TILES):
+            acc = product(t, whole, "acc%d" % t)
+            fetch(gv[t][:], vel_sb[t], whole, VEL_FACTOR)
+            grad = vel_sb[t][:, :S]
+            nc.scalar.activation(out=grad, in_=acc[:], func=COPY, scale=GRAD_FACTOR)
+            nc.gpsimd.tensor_tensor(step[:], gv[t][:], grad, ADD)
+            fetch(gp[t][:], par_sb[t], whole, 1.0)
+            if t == last:
+                nc.vector.tensor_tensor(par_sb[t][:].indirect(ent_sb[:]), step[:], gp[t][:], ADD)
+            else:
+                nc.gpsimd.tensor_tensor(gv[t][:], step[:], gp[t][:], ADD)
+                scatter(t, whole, gv[t][:])
             nc.sync.dma_start(out=out_rows[t], in_=par_sb[t][:])

@@ -129,7 +129,6 @@ def tile_picked_snag_none_p_kernel(tc, x_words, x_scales, w1, par, vel, offs, en
         scatter(1, whole, gv[1][:])
         nc.sync.dma_start(out=out_rows[1], in_=par_sb[1][:])
 
-        last = TILES - 1
         for t in range(2, TILES):
             acc = product(t, whole, "acc%d" % t)
             fetch(gv[t][:], vel_sb[t], whole, VEL_FACTOR)
@@ -137,9 +136,6 @@ def tile_picked_snag_none_p_kernel(tc, x_words, x_scales, w1, par, vel, offs, en
             nc.scalar.activation(out=grad, in_=acc[:], func=COPY, scale=GRAD_FACTOR)
             nc.gpsimd.tensor_tensor(step[:], gv[t][:], grad, ADD)
             fetch(gp[t][:], par_sb[t], whole, 1.0)
-            if t == last:
-                nc.vector.tensor_tensor(par_sb[t][:].indirect(ent_sb[:]), step[:], gp[t][:], ADD)
-            else:
-                nc.gpsimd.tensor_tensor(gv[t][:], step[:], gp[t][:], ADD)
-                scatter(t, whole, gv[t][:])
+            nc.gpsimd.tensor_tensor(gv[t][:], step[:], gp[t][:], ADD)
+            scatter(t, whole, gv[t][:])
             nc.sync.dma_start(out=out_rows[t], in_=par_sb[t][:])

@@ -109,10 +109,12 @@ def tile_picked_snag_none_p_kernel(tc, x_words, x_scales, w1, par, vel, offs, en
         whole = slice(0, S)
 
         acc_a = product(0, a, "acc0a")
+        acc_2a = product(2, a, "acc2a")
         acc_b = product(0, b, "acc0b")
         fetch(gv[0][:, a], vel_sb[0], a, VEL_FACTOR)
-        fetch(gv[0][:, b], vel_sb[0], b, VEL_FACTOR)
+        nc.vector.tensor_scalar(gv[0][:, b], vel_sb[0][:].indirect(entries(ent_sb, b)), VEL_FACTOR, 0.0, MULT, ADD)
         nc.vector.scalar_tensor_tensor(step0[:, a], acc_a[:], GRAD_FACTOR, gv[0][:, a], MULT, ADD)
+        nc.scalar.activation(out=vel_sb[0][:, a], in_=acc_2a[:], func=COPY, scale=GRAD_FACTOR)
         nc.vector.tensor_tensor(gp[0][:, a], par_sb[0][:].indirect(entries(ent_sb, a)), step0[:, a], ADD)
         fetch(gp[0][:, b], par_sb[0], b, 1.0)
         nc.vector.scalar_tensor_tensor(step0[:, b], acc_b[:], GRAD_FACTOR, gp[0][:, b], MULT, ADD)
@@ -120,22 +122,31 @@ def tile_picked_snag_none_p_kernel(tc, x_words, x_scales, w1, par, vel, offs, en
 
         acc = product(1, whole, "acc1")
         fetch(gv[1][:], vel_sb[1], whole, VEL_FACTOR)
-        nc.vector.scalar_tensor_tensor(step[:], acc[:], GRAD_FACTOR, gv[1][:], MULT, ADD)
+        for pick in halves:
+            nc.vector.scalar_tensor_tensor(step[:, pick], acc[:, pick], GRAD_FACTOR, gv[1][:, pick], MULT, ADD)
         nc.gpsimd.tensor_tensor(vel_sb[1][:, a], step0[:, b], gv[0][:, b], ADD)
         scatter(0, b, vel_sb[1][:, a])
         nc.sync.dma_start(out=out_rows[0], in_=par_sb[0][:])
-        fetch(gp[1][:], par_sb[1], whole, 1.0)
-        nc.gpsimd.tensor_tensor(gv[1][:], step[:], gp[1][:], ADD)
+        for pick in halves:
+            fetch(gp[1][:, pick], par_sb[1], pick, 1.0)
+            nc.gpsimd.tensor_tensor(gv[1][:, pick], step[:, pick], gp[1][:, pick], ADD)
         scatter(1, whole, gv[1][:])
         nc.sync.dma_start(out=out_rows[1], in_=par_sb[1][:])
 
-        for t in range(2, TILES):
-            acc = product(t, whole, "acc%d" % t)
-            fetch(gv[t][:], vel_sb[t], whole, VEL_FACTOR)
-            grad = vel_sb[t][:, :S]
-            nc.scalar.activation(out=grad, in_=acc[:], func=COPY, scale=GRAD_FACTOR)
-            nc.gpsimd.tensor_tensor(step[:], gv[t][:], grad, ADD)
-            fetch(gp[t][:], par_sb[t], whole, 1.0)
-            nc.gpsimd.tensor_tensor(gv[t][:], step[:], gp[t][:], ADD)
-            scatter(t, whole, gv[t][:])
-            nc.sync.dma_start(out=out_rows[t], in_=par_sb[t][:])
+        acc_2b = product(2, b, "acc2b")
+        fetch(gv[2][:], vel_sb[2], whole, VEL_FACTOR)
+        nc.gpsimd.tensor_tensor(step[:, a], gv[2][:, a], vel_sb[0][:, a], ADD)
+        nc.scalar.activation(out=vel_sb[2][:, a], in_=acc_2b[:], func=COPY, scale=GRAD_FACTOR)
+        nc.gpsimd.tensor_tensor(step[:, b], gv[2][:, b], vel_sb[2][:, a], ADD)
+        fetch(gp[2][:], par_sb[2], whole, 1.0)
+        nc.gpsimd.tensor_tensor(gv[2][:], step[:], gp[2][:], ADD)
+        scatter(2, whole, gv[2][:])
+        nc.sync.dma_start(out=out_rows[2], in_=par_sb[2][:])
+
+        fetch(gv[3][:], vel_sb[3], whole, VEL_FACTOR)
+        grad3 = vel_sb[3][:, :S]
+        nc.scalar.activation(out=grad3, in_=product(3, whole, "acc3")[:], func=COPY, scale=GRAD_FACTOR)
+        nc.gpsimd.tensor_tensor(step[:], gv[3][:], grad3, ADD)
+        fetch(gp[3][:], par_sb[3], whole, 1.0)
+        nc.vector.tensor_tensor(par_sb[3][:].indirect(ent_sb[:]), step[:], gp[3][:], ADD)
+        nc.sync.dma_start(out=out_rows[3], in_=par_sb[3][:])

@@ -51,8 +51,8 @@ def tile_picked_snag_none_p_kernel(tc, x_words, x_scales, w1, par, vel, offs, en
         nc.sync.dma_start(offs_sb[:], offs)
         nc.sync.dma_start(out=w_raw[:], in_=w1.rearrange("(p j) m -> p j m", j=PACK))
         nc.sync.dma_start(out=x_table[:], in_=x_words[0].rearrange("p n r -> p (n r)").bitcast(I32))
-        nc.sync.dma_start(out=vel_sb[0][:], in_=vel_rows[0])
         nc.sync.dma_start(ent_sb[:], ent)
+        nc.sync.dma_start(out=vel_sb[0][:], in_=vel_rows[0])
         nc.sync.dma_start(out=par_sb[0][:], in_=par_rows[0])
         for t in range(1, TILES):
             nc.sync.dma_start(out=vel_sb[t][:], in_=vel_rows[t])

@@ -109,37 +109,40 @@ def tile_picked_snag_none_p_kernel(tc, x_words, x_scales, w1, par, vel, offs, en
         whole = slice(0, S)
 
         acc_a = product(0, a, "acc0a")
-        acc_2a = product(2, a, "acc2a")
+        acc_1a = product(1, a, "acc1a")
         acc_b = product(0, b, "acc0b")
+        acc_1b = product(1, b, "acc1b")
         fetch(gv[0][:, a], vel_sb[0], a, VEL_FACTOR)
         nc.vector.tensor_scalar(gv[0][:, b], vel_sb[0][:].indirect(entries(ent_sb, b)), VEL_FACTOR, 0.0, MULT, ADD)
         nc.vector.scalar_tensor_tensor(step0[:, a], acc_a[:], GRAD_FACTOR, gv[0][:, a], MULT, ADD)
-        nc.scalar.activation(out=vel_sb[0][:, a], in_=acc_2a[:], func=COPY, scale=GRAD_FACTOR)
+        step0b = vel_sb[0][:, S : S + S // 2]
+        nc.vector.scalar_tensor_tensor(step0b, acc_b[:], GRAD_FACTOR, gv[0][:, b], MULT, ADD)
+        nc.scalar.activation(out=vel_sb[0][:, a], in_=acc_1a[:], func=COPY, scale=GRAD_FACTOR)
+        nc.scalar.activation(out=vel_sb[0][:, b], in_=acc_1b[:], func=COPY, scale=GRAD_FACTOR)
         nc.vector.tensor_tensor(gp[0][:, a], par_sb[0][:].indirect(entries(ent_sb, a)), step0[:, a], ADD)
         fetch(gp[0][:, b], par_sb[0], b, 1.0)
-        nc.vector.scalar_tensor_tensor(step0[:, b], acc_b[:], GRAD_FACTOR, gp[0][:, b], MULT, ADD)
         scatter(0, a, gp[0][:, a])
-
-        acc = product(1, whole, "acc1")
-        fetch(gv[1][:], vel_sb[1], whole, VEL_FACTOR)
-        for pick in halves:
-            nc.vector.scalar_tensor_tensor(step[:, pick], acc[:, pick], GRAD_FACTOR, gv[1][:, pick], MULT, ADD)
-        nc.gpsimd.tensor_tensor(vel_sb[1][:, a], step0[:, b], gv[0][:, b], ADD)
-        scatter(0, b, vel_sb[1][:, a])
+        nc.gpsimd.tensor_tensor(gv[0][:, b], step0b, gp[0][:, b], ADD)
+        scatter(0, b, gv[0][:, b])
         nc.sync.dma_start(out=out_rows[0], in_=par_sb[0][:])
+
+        for pick in halves:
+            fetch(gv[1][:, pick], vel_sb[1], pick, VEL_FACTOR)
+            nc.gpsimd.tensor_tensor(step[:, pick], gv[1][:, pick], vel_sb[0][:, pick], ADD)
         for pick in halves:
             fetch(gp[1][:, pick], par_sb[1], pick, 1.0)
             nc.gpsimd.tensor_tensor(gv[1][:, pick], step[:, pick], gp[1][:, pick], ADD)
         scatter(1, whole, gv[1][:])
         nc.sync.dma_start(out=out_rows[1], in_=par_sb[1][:])
 
-        acc_2b = product(2, b, "acc2b")
+        acc = product(2, whole, "acc2")
         fetch(gv[2][:], vel_sb[2], whole, VEL_FACTOR)
-        nc.gpsimd.tensor_tensor(step[:, a], gv[2][:, a], vel_sb[0][:, a], ADD)
-        nc.scalar.activation(out=vel_sb[2][:, a], in_=acc_2b[:], func=COPY, scale=GRAD_FACTOR)
-        nc.gpsimd.tensor_tensor(step[:, b], gv[2][:, b], vel_sb[2][:, a], ADD)
-        fetch(gp[2][:], par_sb[2], whole, 1.0)
-        nc.gpsimd.tensor_tensor(gv[2][:], step[:], gp[2][:], ADD)
+        for pick in halves:
+            nc.scalar.activation(out=vel_sb[2][:, pick], in_=acc[:, pick], func=COPY, scale=GRAD_FACTOR)
+            nc.gpsimd.tensor_tensor(step[:, pick], gv[2][:, pick], vel_sb[2][:, pick], ADD)
+        for pick in halves:
+            fetch(gp[2][:, pick], par_sb[2], pick, 1.0)
+            nc.gpsimd.tensor_tensor(gv[2][:, pick], step[:, pick], gp[2][:, pick], ADD)
         scatter(2, whole, gv[2][:])
         nc.sync.dma_start(out=out_rows[2], in_=par_sb[2][:])
 

@@ -20,6 +20,8 @@ P = 128
 PACK = 4
 TILES = N // P
 SPLIT = 64
+HALF = S // 2
+JOINT = 256
 VEL_FACTOR = 0.75 * 0.75
 GRAD_FACTOR = -(0.75 * 0.25 + 0.25)
 
@@ -81,11 +83,10 @@ def tile_picked_snag_none_p_kernel(tc, x_words, x_scales, w1, par, vel, offs, en
         for pick in halves:
             nc.vector.tensor_copy(x_codes[:, pick], x_table[:].bitcast(U32).indirect(entries(offs_sb, pick)))
 
-        def product(t, pick, name):
+        def product(t, pick, acc):
             cols = slice(t * P, (t + 1) * P)
-            acc = psum.tile([P, pick.stop - pick.start], F32, name=name)
             nc.tensor.matmul_mx(
-                out=acc[:],
+                out=acc,
                 lhsT=w_codes[:, cols].bitcast(FP8X4),
                 lhsT_scale=w_scale[:, cols],
                 rhs=x_codes[:, pick].bitcast(FP8X4),
@@ -93,7 +94,6 @@ def tile_picked_snag_none_p_kernel(tc, x_words, x_scales, w1, par, vel, offs, en
                 start=True,
                 stop=True,
             )
-            return acc
 
         def fetch(dst, table, pick, factor):
             nc.scalar.activation(out=dst, in_=table[:].indirect(entries(ent_sb, pick)), func=COPY, scale=factor)
@@ -104,51 +104,64 @@ def tile_picked_snag_none_p_kernel(tc, x_words, x_scales, w1, par, vel, offs, en
         gv = [keep.tile([P, S], F32, name="gv%d" % t) for t in range(TILES)]
         gp = [keep.tile([P, S], F32, name="gp%d" % t) for t in range(TILES)]
         step = keep.tile([P, S], F32, name="step")
-        step0 = keep.tile([P, S], F32, name="step0")
+        step0a = keep.tile([P, HALF], F32, name="step0a")
+        picked = keep.tile([P, HALF + S], F32, name="picked")
+        summed = keep.tile([P, HALF + S], F32, name="summed")
+        acc0a = psum.tile([P, HALF], F32, name="acc0a")
+        acc0b = psum.tile([P, HALF], F32, name="acc0b")
+        acc2a = psum.tile([P, HALF], F32, name="acc2a")
+        acc2b = psum.tile([P, HALF], F32, name="acc2b")
+        acc1 = psum.tile([P, S], F32, name="acc1")
+        acc3 = psum.tile([P, S], F32, name="acc3")
         a, b = halves
         whole = slice(0, S)
+        grad2a = vel_sb[0][:, a]
+        terms = vel_sb[0][:, S : S + HALF + JOINT]
 
-        acc_a = product(0, a, "acc0a")
-        acc_1a = product(1, a, "acc1a")
-        acc_b = product(0, b, "acc0b")
-        acc_1b = product(1, b, "acc1b")
+        product(0, a, acc0a[:])
+        product(1, a, acc1[:, a])
+        product(0, b, acc0b[:])
+        product(2, a, acc2a[:])
         fetch(gv[0][:, a], vel_sb[0], a, VEL_FACTOR)
         nc.vector.tensor_scalar(gv[0][:, b], vel_sb[0][:].indirect(entries(ent_sb, b)), VEL_FACTOR, 0.0, MULT, ADD)
-        nc.vector.scalar_tensor_tensor(step0[:, a], acc_a[:], GRAD_FACTOR, gv[0][:, a], MULT, ADD)
-        step0b = vel_sb[0][:, S : S + S // 2]
-        nc.vector.scalar_tensor_tensor(step0b, acc_b[:], GRAD_FACTOR, gv[0][:, b], MULT, ADD)
-        nc.scalar.activation(out=vel_sb[0][:, a], in_=acc_1a[:], func=COPY, scale=GRAD_FACTOR)
-        nc.scalar.activation(out=vel_sb[0][:, b], in_=acc_1b[:], func=COPY, scale=GRAD_FACTOR)
-        nc.vector.tensor_tensor(gp[0][:, a], par_sb[0][:].indirect(entries(ent_sb, a)), step0[:, a], ADD)
-        fetch(gp[0][:, b], par_sb[0], b, 1.0)
+        nc.vector.scalar_tensor_tensor(step0a[:], acc0a[:], GRAD_FACTOR, gv[0][:, a], MULT, ADD)
+        nc.vector.scalar_tensor_tensor(terms[:, :HALF], acc0b[:], GRAD_FACTOR, gv[0][:, b], MULT, ADD)
+        nc.scalar.activation(out=terms[:, HALF:], in_=acc1[:, :JOINT], func=COPY, scale=GRAD_FACTOR)
+        product(1, b, acc1[:, b])
+        nc.scalar.activation(out=grad2a, in_=acc2a[:], func=COPY, scale=GRAD_FACTOR)
+        nc.vector.tensor_tensor(gp[0][:, a], par_sb[0][:].indirect(entries(ent_sb, a)), step0a[:], ADD)
+        fetch(picked[:, :HALF], par_sb[0], b, 1.0)
         scatter(0, a, gp[0][:, a])
-        nc.gpsimd.tensor_tensor(gv[0][:, b], step0b, gp[0][:, b], ADD)
-        scatter(0, b, gv[0][:, b])
-        nc.sync.dma_start(out=out_rows[0], in_=par_sb[0][:])
 
+        vel1 = picked[:, HALF:]
+        step1 = summed[:, HALF:]
         for pick in halves:
-            fetch(gv[1][:, pick], vel_sb[1], pick, VEL_FACTOR)
-            nc.gpsimd.tensor_tensor(step[:, pick], gv[1][:, pick], vel_sb[0][:, pick], ADD)
+            fetch(vel1[:, pick], vel_sb[1], pick, VEL_FACTOR)
+        nc.vector.scalar_tensor_tensor(step1[:, JOINT:], acc1[:, JOINT:], GRAD_FACTOR, vel1[:, JOINT:], MULT, ADD)
+        nc.gpsimd.tensor_tensor(summed[:, : HALF + JOINT], terms, picked[:, : HALF + JOINT], ADD)
+        scatter(0, b, summed[:, :HALF])
+        nc.sync.dma_start(out=out_rows[0], in_=par_sb[0][:])
         for pick in halves:
             fetch(gp[1][:, pick], par_sb[1], pick, 1.0)
-            nc.gpsimd.tensor_tensor(gv[1][:, pick], step[:, pick], gp[1][:, pick], ADD)
+            nc.gpsimd.tensor_tensor(gv[1][:, pick], step1[:, pick], gp[1][:, pick], ADD)
         scatter(1, whole, gv[1][:])
         nc.sync.dma_start(out=out_rows[1], in_=par_sb[1][:])
 
-        acc = product(2, whole, "acc2")
+        product(2, b, acc2b[:])
         fetch(gv[2][:], vel_sb[2], whole, VEL_FACTOR)
-        for pick in halves:
-            nc.scalar.activation(out=vel_sb[2][:, pick], in_=acc[:, pick], func=COPY, scale=GRAD_FACTOR)
-            nc.gpsimd.tensor_tensor(step[:, pick], gv[2][:, pick], vel_sb[2][:, pick], ADD)
+        nc.gpsimd.tensor_tensor(step[:, a], gv[2][:, a], grad2a, ADD)
+        nc.scalar.activation(out=vel_sb[2][:, a], in_=acc2b[:], func=COPY, scale=GRAD_FACTOR)
+        nc.gpsimd.tensor_tensor(step[:, b], gv[2][:, b], vel_sb[2][:, a], ADD)
         for pick in halves:
             fetch(gp[2][:, pick], par_sb[2], pick, 1.0)
             nc.gpsimd.tensor_tensor(gv[2][:, pick], step[:, pick], gp[2][:, pick], ADD)
         scatter(2, whole, gv[2][:])
         nc.sync.dma_start(out=out_rows[2], in_=par_sb[2][:])
 
+        product(3, whole, acc3[:])
         fetch(gv[3][:], vel_sb[3], whole, VEL_FACTOR)
         grad3 = vel_sb[3][:, :S]
-        nc.scalar.activation(out=grad3, in_=product(3, whole, "acc3")[:], func=COPY, scale=GRAD_FACTOR)
+        nc.scalar.activation(out=grad3, in_=acc3[:], func=COPY, scale=GRAD_FACTOR)
         nc.gpsimd.tensor_tensor(step[:], gv[3][:], grad3, ADD)
         fetch(gp[3][:], par_sb[3], whole, 1.0)
         nc.vector.tensor_tensor(par_sb[3][:].indirect(ent_sb[:]), step[:], gp[3][:], ADD)

@@ -22,6 +22,7 @@ TILES = N // P
 SPLIT = 64
 HALF = S // 2
 JOINT = 256
+EARLY = 224
 VEL_FACTOR = 0.75 * 0.75
 GRAD_FACTOR = -(0.75 * 0.25 + 0.25)
 
@@ -132,20 +133,23 @@ def tile_picked_snag_none_p_kernel(tc, x_words, x_scales, w1, par, vel, offs, en
         nc.vector.tensor_tensor(gp[0][:, a], par_sb[0][:].indirect(entries(ent_sb, a)), step0a[:], ADD)
         fetch(picked[:, :HALF], par_sb[0], b, 1.0)
         scatter(0, a, gp[0][:, a])
+        nc.gpsimd.tensor_tensor(summed[:, :EARLY], terms[:, :EARLY], picked[:, :EARLY], ADD)
 
         vel1 = picked[:, HALF:]
         step1 = summed[:, HALF:]
         for pick in halves:
             fetch(vel1[:, pick], vel_sb[1], pick, VEL_FACTOR)
         nc.vector.scalar_tensor_tensor(step1[:, JOINT:], acc1[:, JOINT:], GRAD_FACTOR, vel1[:, JOINT:], MULT, ADD)
-        nc.gpsimd.tensor_tensor(summed[:, : HALF + JOINT], terms, picked[:, : HALF + JOINT], ADD)
+        nc.gpsimd.tensor_tensor(summed[:, EARLY : HALF + JOINT], terms[:, EARLY:], picked[:, EARLY : HALF + JOINT], ADD)
         scatter(0, b, summed[:, :HALF])
-        nc.sync.dma_start(out=out_rows[0], in_=par_sb[0][:])
+        for cols in (slice(0, U // 2), slice(U // 2, U)):
+            nc.sync.dma_start(out=out_rows[0][:, cols], in_=par_sb[0][:, cols])
         for pick in halves:
             fetch(gp[1][:, pick], par_sb[1], pick, 1.0)
             nc.gpsimd.tensor_tensor(gv[1][:, pick], step1[:, pick], gp[1][:, pick], ADD)
         scatter(1, whole, gv[1][:])
-        nc.sync.dma_start(out=out_rows[1], in_=par_sb[1][:])
+        for cols in (slice(0, U // 2), slice(U // 2, U)):
+            nc.sync.dma_start(out=out_rows[1][:, cols], in_=par_sb[1][:, cols])
 
         product(2, b, acc2b[:])
         fetch(gv[2][:], vel_sb[2], whole, VEL_FACTOR)
@@ -156,7 +160,8 @@ def tile_picked_snag_none_p_kernel(tc, x_words, x_scales, w1, par, vel, offs, en
             fetch(gp[2][:, pick], par_sb[2], pick, 1.0)
             nc.gpsimd.tensor_tensor(gv[2][:, pick], step[:, pick], gp[2][:, pick], ADD)
         scatter(2, whole, gv[2][:])
-        nc.sync.dma_start(out=out_rows[2], in_=par_sb[2][:])
+        for cols in (slice(0, U // 2), slice(U // 2, U)):
+            nc.sync.dma_start(out=out_rows[2][:, cols], in_=par_sb[2][:, cols])
 
         product(3, whole, acc3[:])
         fetch(gv[3][:], vel_sb[3], whole, VEL_FACTOR)

@@ -142,14 +142,12 @@ def tile_picked_snag_none_p_kernel(tc, x_words, x_scales, w1, par, vel, offs, en
         nc.vector.scalar_tensor_tensor(step1[:, JOINT:], acc1[:, JOINT:], GRAD_FACTOR, vel1[:, JOINT:], MULT, ADD)
         nc.gpsimd.tensor_tensor(summed[:, EARLY : HALF + JOINT], terms[:, EARLY:], picked[:, EARLY : HALF + JOINT], ADD)
         scatter(0, b, summed[:, :HALF])
-        for cols in (slice(0, U // 2), slice(U // 2, U)):
-            nc.sync.dma_start(out=out_rows[0][:, cols], in_=par_sb[0][:, cols])
+        nc.sync.dma_start(out=out_rows[0], in_=par_sb[0][:])
         for pick in halves:
             fetch(gp[1][:, pick], par_sb[1], pick, 1.0)
             nc.gpsimd.tensor_tensor(gv[1][:, pick], step1[:, pick], gp[1][:, pick], ADD)
         scatter(1, whole, gv[1][:])
-        for cols in (slice(0, U // 2), slice(U // 2, U)):
-            nc.sync.dma_start(out=out_rows[1][:, cols], in_=par_sb[1][:, cols])
+        nc.sync.dma_start(out=out_rows[1], in_=par_sb[1][:])
 
         product(2, b, acc2b[:])
         fetch(gv[2][:], vel_sb[2], whole, VEL_FACTOR)
@@ -160,8 +158,7 @@ def tile_picked_snag_none_p_kernel(tc, x_words, x_scales, w1, par, vel, offs, en
             fetch(gp[2][:, pick], par_sb[2], pick, 1.0)
             nc.gpsimd.tensor_tensor(gv[2][:, pick], step[:, pick], gp[2][:, pick], ADD)
         scatter(2, whole, gv[2][:])
-        for cols in (slice(0, U // 2), slice(U // 2, U)):
-            nc.sync.dma_start(out=out_rows[2][:, cols], in_=par_sb[2][:, cols])
+        nc.sync.dma_start(out=out_rows[2], in_=par_sb[2][:])
 
         product(3, whole, acc3[:])
         fetch(gv[3][:], vel_sb[3], whole, VEL_FACTOR)

@@ -150,7 +150,8 @@ def tile_picked_snag_none_p_kernel(tc, x_words, x_scales, w1, par, vel, offs, en
         nc.sync.dma_start(out=out_rows[1], in_=par_sb[1][:])
 
         product(2, b, acc2b[:])
-        fetch(gv[2][:], vel_sb[2], whole, VEL_FACTOR)
+        for pick in halves:
+            fetch(gv[2][:, pick], vel_sb[2], pick, VEL_FACTOR)
         nc.gpsimd.tensor_tensor(step[:, a], gv[2][:, a], grad2a, ADD)
         nc.scalar.activation(out=vel_sb[2][:, a], in_=acc2b[:], func=COPY, scale=GRAD_FACTOR)
         nc.gpsimd.tensor_tensor(step[:, b], gv[2][:, b], vel_sb[2][:, a], ADD)

@@ -23,6 +23,7 @@ SPLIT = 64
 HALF = S // 2
 JOINT = 256
 EARLY = 224
+ROW0 = 112
 VEL_FACTOR = 0.75 * 0.75
 GRAD_FACTOR = -(0.75 * 0.25 + 0.25)
 
@@ -31,58 +32,69 @@ def tile_picked_snag_none_p_kernel(tc, x_words, x_scales, w1, par, vel, offs, en
     nc = tc.nc
     with ExitStack() as ctx:
         keep = ctx.enter_context(tc.tile_pool(name="keep", bufs=1))
+        first = ctx.enter_context(tc.tile_pool(name="first", bufs=1))
+        second = ctx.enter_context(tc.tile_pool(name="second", bufs=1))
         psum = ctx.enter_context(tc.psum_pool(name="psum", bufs=1))
 
         offs_sb = keep.tile([P, S // 16], U16, name="offs_sb")
         ent_sb = keep.tile([P, S // 16], U16, name="ent_sb")
-        w_raw = keep.tile([P, PACK, N], F32, name="w_raw")
-        x_table = keep.tile([P, T], I32, name="x_table")
-        xs_table = keep.tile([P, T], U8, name="xs_table")
-        vel_sb = [keep.tile([P, U], F32, name="vel_sb%d" % t) for t in range(TILES)]
-        par_sb = [keep.tile([P, U], F32, name="par_sb%d" % t) for t in range(TILES)]
-
-        nc.vector.memset(xs_table[:].bitcast(I32), 0)
-        for q in range(4):
-            nc.sync.dma_start(
-                out=xs_table[32 * q : 32 * q + 4, :].bitcast(I32),
-                in_=x_scales[0, 4 * q : 4 * q + 4, :].bitcast(I32),
-            )
-
         vel_rows = vel.rearrange("(p t) u -> t p u", t=TILES)
         par_rows = par.rearrange("(p t) u -> t p u", t=TILES)
         out_rows = out.rearrange("(p t) u -> t p u", t=TILES)
+
+        xs_table = first.tile([P, T], U8, name="xs_table", offset=4 * U - T // 2)
+        nc.vector.memset(xs_table[:96, :].bitcast(I32), 0)
+        nc.vector.memset(xs_table[96:ROW0, :].bitcast(I32), 0)
+        nc.sync.dma_start(out=xs_table[ROW0:, :].bitcast(I32), in_=x_scales[0].bitcast(I32))
         nc.sync.dma_start(offs_sb[:], offs)
+        w_raw = keep.tile([P, PACK, N], F32, name="w_raw", tag="after_w")
         nc.sync.dma_start(out=w_raw[:], in_=w1.rearrange("(p j) m -> p j m", j=PACK))
+        x_table = keep.tile([P, T], I32, name="x_table", tag="after_x")
         nc.sync.dma_start(out=x_table[:], in_=x_words[0].rearrange("p n r -> p (n r)").bitcast(I32))
         nc.sync.dma_start(ent_sb[:], ent)
-        nc.sync.dma_start(out=vel_sb[0][:], in_=vel_rows[0])
-        nc.sync.dma_start(out=par_sb[0][:], in_=par_rows[0])
-        for t in range(1, TILES):
-            nc.sync.dma_start(out=vel_sb[t][:], in_=vel_rows[t])
-            nc.sync.dma_start(out=par_sb[t][:], in_=par_rows[t])
 
+        xs_picked = keep.tile([P, S], U8, name="xs_picked", tag="after_picked")
+        nc.vector.tensor_copy(xs_picked[:], xs_table[:].indirect(offs_sb[:]))
         x_scale = keep.tile([P, S], U8, name="x_scale", align_bytes=64)
-        nc.vector.tensor_copy(x_scale[:], xs_table[:].indirect(offs_sb[:]))
+        nc.vector.memset(x_scale[:].bitcast(I32), 0)
+        for q in range(4):
+            nc.sync.dma_start(
+                out=x_scale[32 * q : 32 * q + 4, :].bitcast(I32),
+                in_=xs_picked[ROW0 + 4 * q : ROW0 + 4 * q + 4, :].bitcast(I32),
+            )
+        vel0 = first.tile([P, U], F32, name="vel0", offset=0)
+        nc.sync.dma_start(out=vel0[:], in_=vel_rows[0])
+        par0 = first.tile([P, U], F32, name="par0", offset=4 * U)
+        nc.sync.dma_start(out=par0[:], in_=par_rows[0])
 
-        grouped = keep.tile([P, TILES, P, PACK], BF16, name="grouped", align_bytes=64)
+        grouped = second.tile([P, TILES, P, PACK], BF16, name="grouped", offset=0, align_bytes=64)
         w_dst = grouped[:].rearrange("p t m j -> p m j t")
         w_src = w_raw[:].rearrange("p j (m t) -> p m j t", t=TILES)
         nc.vector.tensor_copy(out=w_dst[:, :SPLIT], in_=w_src[:, :SPLIT])
         nc.scalar.copy(out=w_dst[:, SPLIT:], in_=w_src[:, SPLIT:])
+        vel1_sb = keep.tile([P, U], F32, name="vel1_sb", tag="after_w")
+        nc.sync.dma_start(out=vel1_sb[:], in_=vel_rows[1])
         w_codes = keep.tile([P, N], U32, name="w_codes", align_bytes=64)
         w_scale = keep.tile([P, N], U8, name="w_scale", align_bytes=64)
         nc.vector.quantize_mx(
             out=w_codes[:].bitcast(FP8X4), scales=w_scale[:], in_=grouped[:].rearrange("p t m j -> p (t m j)")
         )
+        par1 = second.tile([P, U], F32, name="par1", offset=4 * S, align_bytes=64)
+        nc.sync.dma_start(out=par1[:], in_=par_rows[1])
 
         halves = (slice(0, S // 2), slice(S // 2, S))
 
         def entries(tile, pick):
             return tile[:, pick.start // 16 : pick.stop // 16]
 
-        x_codes = keep.tile([P, S], U32, name="x_codes", align_bytes=64)
+        x_codes = second.tile([P, S], U32, name="x_codes", offset=0, align_bytes=64)
         for pick in halves:
             nc.vector.tensor_copy(x_codes[:, pick], x_table[:].bitcast(U32).indirect(entries(offs_sb, pick)))
+
+        vel2 = keep.tile([P, U], F32, name="vel2", tag="after_picked")
+        nc.sync.dma_start(out=vel2[:], in_=vel_rows[2])
+        par2 = keep.tile([P, U], F32, name="par2", tag="after_x")
+        nc.sync.dma_start(out=par2[:], in_=par_rows[2])
 
         def product(t, pick, acc):
             cols = slice(t * P, (t + 1) * P)
@@ -102,10 +114,10 @@ def tile_picked_snag_none_p_kernel(tc, x_words, x_scales, w1, par, vel, offs, en
         def scatter(t, pick, values):
             nc.vector.tensor_copy(par_sb[t][:].indirect(entries(ent_sb, pick)), values)
 
-        gv = [keep.tile([P, S], F32, name="gv%d" % t) for t in range(TILES)]
+        gv = [keep.tile([P, S], F32, name="gv%d" % t, tag="gv%d" % t) for t in range(TILES)]
         gp = [keep.tile([P, S], F32, name="gp%d" % t) for t in range(TILES)]
         step = keep.tile([P, S], F32, name="step")
-        step0a = keep.tile([P, HALF], F32, name="step0a")
+        step0a = keep.tile([P, HALF], F32, name="step0a", tag="after_step")
         picked = keep.tile([P, HALF + S], F32, name="picked")
         summed = keep.tile([P, HALF + S], F32, name="summed")
         acc0a = psum.tile([P, HALF], F32, name="acc0a")
@@ -115,6 +127,8 @@ def tile_picked_snag_none_p_kernel(tc, x_words, x_scales, w1, par, vel, offs, en
         acc1 = psum.tile([P, S], F32, name="acc1")
         acc3 = psum.tile([P, S], F32, name="acc3")
         a, b = halves
+        vel_sb = [vel0, vel1_sb, vel2]
+        par_sb = [par0, par1, par2]
         whole = slice(0, S)
         grad2a = vel_sb[0][:, a]
         terms = vel_sb[0][:, S : S + HALF + JOINT]
@@ -131,6 +145,12 @@ def tile_picked_snag_none_p_kernel(tc, x_words, x_scales, w1, par, vel, offs, en
         product(1, b, acc1[:, b])
         nc.scalar.activation(out=grad2a, in_=acc2a[:], func=COPY, scale=GRAD_FACTOR)
         nc.vector.tensor_tensor(gp[0][:, a], par_sb[0][:].indirect(entries(ent_sb, a)), step0a[:], ADD)
+        vel3 = keep.tile([P, U], F32, name="vel3", tag="gv0")
+        nc.sync.dma_start(out=vel3[:], in_=vel_rows[3])
+        par3 = keep.tile([P, U], F32, name="par3", tag="after_step")
+        nc.sync.dma_start(out=par3[:], in_=par_rows[3])
+        vel_sb.append(vel3)
+        par_sb.append(par3)
         fetch(picked[:, :HALF], par_sb[0], b, 1.0)
         scatter(0, a, gp[0][:, a])
         nc.gpsimd.tensor_tensor(summed[:, :EARLY], terms[:, :EARLY], picked[:, :EARLY], ADD)

@@ -19,7 +19,7 @@ COPY = mybir.ActivationFunctionType.Copy
 P = 128
 PACK = 4
 TILES = N // P
-SPLIT = 64
+SPLIT = 88
 HALF = S // 2
 JOINT = 256
 EARLY = 224
@@ -45,7 +45,7 @@ def tile_picked_snag_none_p_kernel(tc, x_words, x_scales, w1, par, vel, offs, en
         xs_table = first.tile([P, T], U8, name="xs_table", offset=4 * U - T // 2)
         nc.vector.memset(xs_table[:96, :].bitcast(I32), 0)
         nc.vector.memset(xs_table[96:ROW0, :].bitcast(I32), 0)
-        nc.sync.dma_start(out=xs_table[ROW0:, :].bitcast(I32), in_=x_scales[0].bitcast(I32))
+        nc.scalar.dma_start(out=xs_table[ROW0:, :].bitcast(I32), in_=x_scales[0].bitcast(I32))
         nc.sync.dma_start(offs_sb[:], offs)
         w_raw = keep.tile([P, PACK, N], F32, name="w_raw", tag="after_w")
         nc.sync.dma_start(out=w_raw[:], in_=w1.rearrange("(p j) m -> p j m", j=PACK))

from contextlib import ExitStack

import concourse.mybir as mybir

K, T, S, N, U = 512, 2048, 512, 512, 1024
FLOPS = 2 * K * N * S

F32 = mybir.dt.float32
BF16 = mybir.dt.bfloat16
I32 = mybir.dt.int32
U32 = mybir.dt.uint32
U16 = mybir.dt.uint16
U8 = mybir.dt.uint8
FP8X4 = mybir.dt.float8_e4m3fn_x4
MULT = mybir.AluOpType.mult
ADD = mybir.AluOpType.add
COPY = mybir.ActivationFunctionType.Copy

P = 128
PACK = 4
TILES = N // P
SPLIT = 88
HALF = S // 2
JOINT = 256
EARLY = 224
ROW0 = 112
VEL_FACTOR = 0.75 * 0.75
GRAD_FACTOR = -(0.75 * 0.25 + 0.25)


def tile_picked_snag_none_p_kernel(tc, x_words, x_scales, w1, par, vel, offs, ent, out):
    nc = tc.nc
    with ExitStack() as ctx:
        keep = ctx.enter_context(tc.tile_pool(name="keep", bufs=1))
        first = ctx.enter_context(tc.tile_pool(name="first", bufs=1))
        second = ctx.enter_context(tc.tile_pool(name="second", bufs=1))
        psum = ctx.enter_context(tc.psum_pool(name="psum", bufs=1))

        offs_sb = keep.tile([P, S // 16], U16, name="offs_sb")
        ent_sb = keep.tile([P, S // 16], U16, name="ent_sb")
        vel_rows = vel.rearrange("(p t) u -> t p u", t=TILES)
        par_rows = par.rearrange("(p t) u -> t p u", t=TILES)
        out_rows = out.rearrange("(p t) u -> t p u", t=TILES)

        xs_table = first.tile([P, T], U8, name="xs_table", offset=4 * U - T // 2)
        nc.vector.memset(xs_table[:96, :].bitcast(I32), 0)
        nc.vector.memset(xs_table[96:ROW0, :].bitcast(I32), 0)
        nc.scalar.dma_start(out=xs_table[ROW0:, :].bitcast(I32), in_=x_scales[0].bitcast(I32))
        nc.sync.dma_start(offs_sb[:], offs)
        w_raw = keep.tile([P, PACK, N], F32, name="w_raw", tag="after_w")
        nc.sync.dma_start(out=w_raw[:], in_=w1.rearrange("(p j) m -> p j m", j=PACK))
        x_table = keep.tile([P, T], I32, name="x_table", tag="after_x")
        nc.sync.dma_start(out=x_table[:], in_=x_words[0].rearrange("p n r -> p (n r)").bitcast(I32))
        nc.sync.dma_start(ent_sb[:], ent)

        xs_picked = keep.tile([P, S], U8, name="xs_picked", tag="after_picked")
        nc.vector.tensor_copy(xs_picked[:], xs_table[:].indirect(offs_sb[:]))
        x_scale = keep.tile([P, S], U8, name="x_scale", align_bytes=64)
        nc.vector.memset(x_scale[:].bitcast(I32), 0)
        for q in range(4):
            nc.sync.dma_start(
                out=x_scale[32 * q : 32 * q + 4, :].bitcast(I32),
                in_=xs_picked[ROW0 + 4 * q : ROW0 + 4 * q + 4, :].bitcast(I32),
            )
        vel0 = first.tile([P, U], F32, name="vel0", offset=0)
        nc.sync.dma_start(out=vel0[:], in_=vel_rows[0])
        par0 = first.tile([P, U], F32, name="par0", offset=4 * U)
        nc.sync.dma_start(out=par0[:], in_=par_rows[0])

        grouped = second.tile([P, TILES, P, PACK], BF16, name="grouped", offset=0, align_bytes=64)
        w_dst = grouped[:].rearrange("p t m j -> p m j t")
        w_src = w_raw[:].rearrange("p j (m t) -> p m j t", t=TILES)
        nc.vector.tensor_copy(out=w_dst[:, :SPLIT], in_=w_src[:, :SPLIT])
        nc.scalar.copy(out=w_dst[:, SPLIT:], in_=w_src[:, SPLIT:])
        vel1_sb = keep.tile([P, U], F32, name="vel1_sb", tag="after_w")
        nc.sync.dma_start(out=vel1_sb[:], in_=vel_rows[1])
        w_codes = keep.tile([P, N], U32, name="w_codes", align_bytes=64)
        w_scale = keep.tile([P, N], U8, name="w_scale", align_bytes=64)
        nc.vector.quantize_mx(
            out=w_codes[:].bitcast(FP8X4), scales=w_scale[:], in_=grouped[:].rearrange("p t m j -> p (t m j)")
        )
        par1 = second.tile([P, U], F32, name="par1", offset=4 * S, align_bytes=64)
        nc.sync.dma_start(out=par1[:], in_=par_rows[1])

        halves = (slice(0, S // 2), slice(S // 2, S))

        def entries(tile, pick):
            return tile[:, pick.start // 16 : pick.stop // 16]

        x_codes = second.tile([P, S], U32, name="x_codes", offset=0, align_bytes=64)
        for pick in halves:
            nc.vector.tensor_copy(x_codes[:, pick], x_table[:].bitcast(U32).indirect(entries(offs_sb, pick)))

        vel2 = keep.tile([P, U], F32, name="vel2", tag="after_picked")
        nc.sync.dma_start(out=vel2[:], in_=vel_rows[2])
        par2 = keep.tile([P, U], F32, name="par2", tag="after_x")
        nc.sync.dma_start(out=par2[:], in_=par_rows[2])

        def product(t, pick, acc):
            cols = slice(t * P, (t + 1) * P)
            nc.tensor.matmul_mx(
                out=acc,
                lhsT=w_codes[:, cols].bitcast(FP8X4),
                lhsT_scale=w_scale[:, cols],
                rhs=x_codes[:, pick].bitcast(FP8X4),
                rhs_scale=x_scale[:, pick],
                start=True,
                stop=True,
            )

        def fetch(dst, table, pick, factor):
            nc.scalar.activation(out=dst, in_=table[:].indirect(entries(ent_sb, pick)), func=COPY, scale=factor)

        def scatter(t, pick, values):
            nc.vector.tensor_copy(par_sb[t][:].indirect(entries(ent_sb, pick)), values)

        gv = [keep.tile([P, S], F32, name="gv%d" % t, tag="gv%d" % t) for t in range(TILES)]
        gp = [keep.tile([P, S], F32, name="gp%d" % t) for t in range(TILES)]
        step = keep.tile([P, S], F32, name="step")
        step0a = keep.tile([P, HALF], F32, name="step0a", tag="after_step")
        picked = keep.tile([P, HALF + S], F32, name="picked")
        summed = keep.tile([P, HALF + S], F32, name="summed")
        acc0a = psum.tile([P, HALF], F32, name="acc0a")
        acc0b = psum.tile([P, HALF], F32, name="acc0b")
        acc2a = psum.tile([P, HALF], F32, name="acc2a")
        acc2b = psum.tile([P, HALF], F32, name="acc2b")
        acc1 = psum.tile([P, S], F32, name="acc1")
        acc3 = psum.tile([P, S], F32, name="acc3")
        a, b = halves
        vel_sb = [vel0, vel1_sb, vel2]
        par_sb = [par0, par1, par2]
        whole = slice(0, S)
        grad2a = vel_sb[0][:, a]
        terms = vel_sb[0][:, S : S + HALF + JOINT]

        product(0, a, acc0a[:])
        product(1, a, acc1[:, a])
        product(0, b, acc0b[:])
        product(2, a, acc2a[:])
        fetch(gv[0][:, a], vel_sb[0], a, VEL_FACTOR)
        nc.vector.tensor_scalar(gv[0][:, b], vel_sb[0][:].indirect(entries(ent_sb, b)), VEL_FACTOR, 0.0, MULT, ADD)
        nc.vector.scalar_tensor_tensor(step0a[:], acc0a[:], GRAD_FACTOR, gv[0][:, a], MULT, ADD)
        nc.vector.scalar_tensor_tensor(terms[:, :HALF], acc0b[:], GRAD_FACTOR, gv[0][:, b], MULT, ADD)
        nc.scalar.activation(out=terms[:, HALF:], in_=acc1[:, :JOINT], func=COPY, scale=GRAD_FACTOR)
        product(1, b, acc1[:, b])
        nc.scalar.activation(out=grad2a, in_=acc2a[:], func=COPY, scale=GRAD_FACTOR)
        nc.vector.tensor_tensor(gp[0][:, a], par_sb[0][:].indirect(entries(ent_sb, a)), step0a[:], ADD)
        vel3 = keep.tile([P, U], F32, name="vel3", tag="gv0")
        nc.sync.dma_start(out=vel3[:], in_=vel_rows[3])
        par3 = keep.tile([P, U], F32, name="par3", tag="after_step")
        nc.sync.dma_start(out=par3[:], in_=par_rows[3])
        vel_sb.append(vel3)
        par_sb.append(par3)
        fetch(picked[:, :HALF], par_sb[0], b, 1.0)
        scatter(0, a, gp[0][:, a])
        nc.gpsimd.tensor_tensor(summed[:, :EARLY], terms[:, :EARLY], picked[:, :EARLY], ADD)

        vel1 = picked[:, HALF:]
        step1 = summed[:, HALF:]
        for pick in halves:
            fetch(vel1[:, pick], vel_sb[1], pick, VEL_FACTOR)
        nc.vector.scalar_tensor_tensor(step1[:, JOINT:], acc1[:, JOINT:], GRAD_FACTOR, vel1[:, JOINT:], MULT, ADD)
        nc.gpsimd.tensor_tensor(summed[:, EARLY : HALF + JOINT], terms[:, EARLY:], picked[:, EARLY : HALF + JOINT], ADD)
        scatter(0, b, summed[:, :HALF])
        nc.sync.dma_start(out=out_rows[0], in_=par_sb[0][:])
        for pick in halves:
            fetch(gp[1][:, pick], par_sb[1], pick, 1.0)
            nc.gpsimd.tensor_tensor(gv[1][:, pick], step1[:, pick], gp[1][:, pick], ADD)
        scatter(1, whole, gv[1][:])
        nc.sync.dma_start(out=out_rows[1], in_=par_sb[1][:])

        product(2, b, acc2b[:])
        for pick in halves:
            fetch(gv[2][:, pick], vel_sb[2], pick, VEL_FACTOR)
        nc.gpsimd.tensor_tensor(step[:, a], gv[2][:, a], grad2a, ADD)
        nc.scalar.activation(out=vel_sb[2][:, a], in_=acc2b[:], func=COPY, scale=GRAD_FACTOR)
        nc.gpsimd.tensor_tensor(step[:, b], gv[2][:, b], vel_sb[2][:, a], ADD)
        for pick in halves:
            fetch(gp[2][:, pick], par_sb[2], pick, 1.0)
            nc.gpsimd.tensor_tensor(gv[2][:, pick], step[:, pick], gp[2][:, pick], ADD)
        scatter(2, whole, gv[2][:])
        nc.sync.dma_start(out=out_rows[2], in_=par_sb[2][:])

        product(3, whole, acc3[:])
        fetch(gv[3][:], vel_sb[3], whole, VEL_FACTOR)
        grad3 = vel_sb[3][:, :S]
        nc.scalar.activation(out=grad3, in_=acc3[:], func=COPY, scale=GRAD_FACTOR)
        nc.gpsimd.tensor_tensor(step[:], gv[3][:], grad3, ADD)
        fetch(gp[3][:], par_sb[3], whole, 1.0)
        nc.vector.tensor_tensor(par_sb[3][:].indirect(ent_sb[:]), step[:], gp[3][:], ADD)
        nc.sync.dma_start(out=out_rows[3], in_=par_sb[3][:])
